import numpy as np, ml_dtypes
CORES = [113,118,241,246]
N = 4
BF = ml_dtypes.bfloat16
def gentries(a):
    return np.ascontiguousarray(a.reshape(8, 16, -1).transpose(0, 2, 1)).reshape(8, -1)
def gtable(e):
    e = np.asarray(e); return np.ascontiguousarray(e.reshape(8, -1, 16).transpose(0, 2, 1)).reshape(128, -1).astype(np.int32)
B, J, CAP, RO, Q = 3072, 4096, 96, 2, 4096
LN, LJ = 2, 12
M = N * CAP; W = B + RO * M
WT = (14 * np.arange(16) + 9)[:, None]
def decode(n):
    C = np.add.accumulate((n * n[..., ::-1]) >> 12, axis=-1)
    x = (C[..., -1:] * np.arange(J)) >> LJ
    return np.add.reduce((C[..., None] <= x[..., None, :]).astype(np.int64), axis=-2)
def combine(x, y, z):
    q = x.shape[-1] // 4
    k = np.concatenate([np.minimum(x[..., :q], y[..., :q]), np.maximum(x[..., q:2 * q], y[..., q:2 * q]), np.abs(x[..., 2 * q:3 * q] - y[..., 2 * q:3 * q]), x[..., 3 * q:] + y[..., 3 * q:]], axis=-1)
    return np.minimum(k, z)
def sizes(c):
    c = np.sort(c, axis=-1); z = np.zeros(c.shape[:-1] + (1,), np.int64)
    return np.diff(np.concatenate([z, c, z + B - 256], axis=-1), axis=-1) + 64
def span(rng, v, share):
    o = rng.integers(0, B, (3, N, 8, 1, 2048)); x, y, z = [np.take_along_axis(v, i, 3) for i in o]
    s = np.sort(np.add.reduce(combine(x, y, z), axis=2), axis=-1)
    m = np.minimum(np.maximum((2048 * share).astype(np.int64), 1), 2048); k = (rng.random((N, 8)) * (2048 - m)).astype(np.int64)
    return np.concatenate([np.take_along_axis(s, k[..., None], 2), np.take_along_axis(s, (k + m - 1)[..., None], 2)], axis=2)
def shares(rng):
    return CAP * N * 2.0 ** -LJ * rng.choice(np.array([0.4, 0.8, 1.0, 1.5]), (N, 8))
def parts(rng):
    e = rng.choice(np.array([0.5, 1.0, 1.0, 2.0]), (N, 8, 16, 1))
    v = np.minimum((256 * rng.random((N, 8, 16, B)) ** e).astype(np.int64), 255)
    n = sizes(rng.integers(0, B - 255, (N, 8, 3))); r = rng.integers(0, 4096, (3, N, 8, RO, J))
    u = (rng.random((N, 8, Q)) < rng.choice(np.array([0.05, 0.2, 0.5]), (N, 8, 1))).astype(np.int64)
    return v, n, span(rng, v, shares(rng)), r, u
def pack(v, n, lim, r, u):
    t = [np.stack([gtable(a.reshape(8, -1)) for a in b]) for b in r]
    return {"bank": np.ascontiguousarray(v.reshape(N, 128, B)).astype(np.float32).astype(BF), "ncl": n.astype(np.int32), "lim": lim.astype(np.int32),
            "ra": t[0], "rb": t[1], "rc": t[2], "used": u.astype(np.int32)}
def goals(rng, k):
    return np.stack([rng.permutation(Q - 1)[:k] + 1 for p in range(N)]) * N + np.arange(N)[:, None]
def keyed(rng, d):
    c = rng.integers(1, 256, (16, d.size)); c[[0, 1, 15]] = rng.integers(40, 101, (3, d.size))
    e = (d - np.add.reduce(c * WT, axis=0)) & (N * Q - 1)
    c[15] += e // 219; e = e % 219; c[0] += e // 9 - 5 * (e % 9); c[1] += 2 * (e % 9)
    return c
def put(rng, v, n, q, g, d):
    s = np.add.accumulate(n[q, g]) - n[q, g]; v[q, g][:, s] = 255; v[q, g][:, s + 1] = 0
    w = rng.permutation(np.setdiff1d(np.arange(B), np.concatenate([s, s + 1])))[:d.size]
    v[q, g][:, w] = keyed(rng, d.reshape(-1)); return w.reshape(d.shape)
def deal(rng, col, at, w):
    o = rng.permutation(np.repeat(np.arange(N), CAP)); at = np.sort(rng.permutation(at)[:M])
    for p in range(N): col[at[o == p]] = w[p]
def play(r, n, q, g, t, col):
    h = J // 4; k = B + t * M; r[:2, q, g, t] = 0; r[2, q, g, t] = (col * 4096 + k - 1) // k
    if t == 0:
        m = n[q, g][3 - decode(n[q, g])[2 * h:3 * h]]; r[1, q, g, 0, 2 * h:3 * h] = (4096 + m - 1) // m
def setup_inputs(rng):
    return pack(*parts(rng))
def setup_inputs_room(rng):
    v, n, lim, r, u = parts(rng); lim[:] = (1500, 2600)
    for q in range(N):
        for g in range(8):
            m = n[q, g]; p = np.concatenate([np.arange(k) for k in m]); live = p >= np.repeat(m // 2, m)
            c = np.where(live, rng.integers(110, 150, (16, B)), rng.integers(0, 90, (16, B)))
            c[0] += (p - np.add.reduce(c * WT, axis=0)) & (N - 1)
            c[:, p == 0] = 0; c[:, p == 1] = 255; v[q, g] = c
            t = rng.choice(np.array([0, 1, CAP - 1, CAP, CAP + 1, 2 * CAP]), N)
            if q == 0: t[1] = (CAP, CAP + 1, CAP - 1, CAP, 0, 1, 2 * CAP, CAP)[g]
            if g == 6: t[2] = 0
            own = np.full(J, -1); own[rng.permutation(J)[:int(np.sum(t))]] = rng.permutation(np.repeat(np.arange(N), t))
            a = decode(m); na = m[a]; nb = m[3 - a]; h = na // 2
            dead = 2 + (rng.random(J) * (h - 2)).astype(np.int64)
            good = h + (own - h) % N + N * (rng.random(J) * ((na - h - N) // N + 1)).astype(np.int64)
            i = np.where(own < 0, dead, good); y = (np.arange(J) < J // 4).astype(np.int64)
            r[0, q, g, 0] = (i * 4096 + na - 1) // na; r[1, q, g, 0] = (y * 4096 + nb - 1) // nb; r[2, q, g, 0] = (4096 + B - 1) // B
    return pack(v, n, lim, r, u)
def setup_inputs_ends(rng):
    v, n, lim, r, u = parts(rng); v[..., 0] = 0; v[..., B - 1] = 255
    for g in range(4):
        n[:, g] = 64; n[:, g, g] = B - 192
    n[:, 5] = n[:, 2]; lim[0, 5] = (1, 4080)
    for g in (0, 2, 4): r[:, :, g] = rng.choice(np.array([0, 1, 4094, 4095]), (3, N, RO, J))
    lim[:, 0] = (0, 4080); lim[:, 2] = (4080, 4080); lim[:, 4] = (0, 0); lim[:, 6, 0] = lim[:, 6, 1]
    r[:, :, 2, 0, J - 1] = 4095; r[2, :, 4, 0, :8] = 0; u[:, 2] = 0; u[:, 4] = 0
    r[2, :, 0, 0, :8] = 0; u[:, 0] = 0
    lim[:, 1] = (1, 4080); lim[:, 3] = (1, 4080); lim[:, 7] = (0, 4079); u[:, 1] = 0; u[:, 3] = 0; u[:, 7] = 0
    full = goals(rng, RO * M).reshape(N, RO, N, CAP)
    grid = goals(rng, M).reshape(N, N, CAP); grid[1:, N - 1, CAP - 1] = grid[1:, 0, 0]
    many = goals(rng, 2 * CAP); at = np.concatenate([np.arange(J // 4, J // 2), np.arange(3 * J // 4, J)])
    for q in range(N):
        w = put(rng, v, n, q, 3, full[:, :, q])
        for t in range(RO):
            col = np.full(J, 1); deal(rng, col, at, w[:, t]); play(r, n, q, 3, t, col)
        i = J // 8 + rng.permutation(J // 8)[:4]; r[0, q, 3, RO - 1, i] = rng.integers(1000, 4096, 4); r[2, q, 3, RO - 1, i] = 0
        w = put(rng, v, n, q, 7, grid[:, q])
        if q == N - 1: w[0, CAP - 1] = 1
        col = np.zeros(J, np.int64); deal(rng, col, np.arange(J), w); play(r, n, q, 7, 0, col)
        w = put(rng, v, n, q, 1, many[(q + 1) % N]); col = np.full(J, 1); k = J // 4
        if q > 0: k += int(rng.integers(0, CAP))
        i = np.sort(rng.permutation(J // 2)[:k]); col[i] = w[rng.integers(0, CAP, k)]; col[i[:CAP]] = w[:CAP]
        col[J // 2 + rng.permutation(J // 2)[:2 * CAP]] = np.tile(w[CAP:], 2); play(r, n, q, 1, 0, col)
    return pack(v, n, lim, r, u)
def setup_inputs_alike(rng):
    v, n, lim, r, u = parts(rng)
    a = rng.integers(1, 255, (8, 16, 3)); tw = np.zeros((16, 1), np.int64); tw[:4, 0] = (1, -1, -1, 1)
    pool = np.concatenate([a, a + tw], axis=2)
    for g in range(1, 8, 2):
        v[:, g] = pool[g][:, rng.integers(0, 6, (N, B))].transpose(1, 0, 2)
        for q in range(N):
            e = np.add.accumulate(n[q, g]); v[q, g][:, e - n[q, g]] = pool[g][:, :1]; v[q, g][:, e - 1] = pool[g][:, 3:4]
    lim[:, 1::2] = (0, 4080); u[:, 1::2] = 0; r[:, :, 1::2, 0, 0] = 0; r[:, :, 1::2, 0, 1] = 4095
    v[:, 2] = v[0, 2]; n[:, 2] = n[0, 2]; lim[:, 2] = lim[0, 2]; r[:, :, 2] = r[:, :1, 2]
    return pack(v, n, lim, r, u)
def setup_inputs_cold(rng):
    v, n, lim, r, u = parts(rng); o = rng.permutation(N); g = int(rng.integers(0, 8))
    lim[o[0]] = (1, 0); lim[o[0], 1::2] = (1600, 1000); lim[o[1]] = (0, 4080)
    lim[:, g] = (1700, 1100); lim[o[0], g] = (2000, 1999); lim[o[1], g] = (4080, 0); u[:, (g + 1) % 8] = 1; u[:, (g + 2) % 8] = 0
    u[o[2], (g + 3) % 8] = 1
    return pack(v, n, lim, r, u)
def setup_inputs_spread(rng):
    v, n, lim, r, u = parts(rng)
    v = np.minimum((np.exp2(8 * rng.random((N, 8, 1, B))) * rng.random((N, 8, 16, B))).astype(np.int64), 255)
    n = sizes(((B - 256) * rng.random((N, 8, 3)) ** 4).astype(np.int64))
    e = rng.choice(np.array([0.5, 1.0, 2.0, 3.0]), (3, N, 8, RO, 1)); r = np.minimum((4096 * rng.random((3, N, 8, RO, J)) ** e).astype(np.int64), 4095)
    u = (rng.random((N, 8, Q)) < 0.8 * rng.random((N, 8, 1))).astype(np.int64)
    return pack(v, n, span(rng, v, shares(rng)), r, u)
def check_inputs(d):
    bad = []; b = np.asarray(d["bank"]).astype(np.float32)
    if not np.all((b >= 0) & (b <= 255) & (b == np.floor(b))): bad.append("bank: whole numbers from 0 to 255")
    for k, lo, hi in (("ncl", 64, B), ("lim", 0, 4080), ("ra", 0, 4095), ("rb", 0, 4095), ("rc", 0, 4095), ("used", 0, 1)):
        if np.min(d[k]) < lo or np.max(d[k]) > hi: bad.append("range of " + k)
    if np.any(np.sum(np.asarray(d["ncl"]).astype(np.int64), axis=-1) != B): bad.append("sums of ncl")
    return bad
def reference(bank, ncl, lim, ra, rb, rc, used):
    v = np.zeros((N, 8, 16, W), np.int32); v[..., :B] = bank.astype(np.float32).astype(np.int32).reshape(N, 8, 16, B)
    n = np.zeros((N, 8, 4 + RO), np.int64); n[:, :, :4] = ncl
    la, lb, lc = [np.stack([gentries(a) for a in b]).astype(np.int64).reshape(N, 8, RO, J) for b in (ra, rb, rc)]
    free = used == 0; lo = lim[:, :, :1]; hi = lim[:, :, 1:]; take = np.take_along_axis
    for t in range(RO):
        s = 4 + t; m = n[:, :, :s].copy(); start = np.add.accumulate(m, axis=2) - m; tot = np.add.reduce(m, axis=2)
        a = decode(m); b = s - 1 - a
        ix = take(start, a, 2) + ((take(m, a, 2) * la[:, :, t]) >> 12)
        iy = take(start, b, 2) + ((take(m, b, 2) * lb[:, :, t]) >> 12)
        iz = (tot[:, :, None] * lc[:, :, t]) >> 12
        x, y, z = [take(v, i[:, :, None, :], 3) for i in (ix, iy, iz)]
        k = combine(x, y, z)
        total = np.add.reduce(k, axis=2); key = np.add.reduce(k * WT, axis=2)
        alive = (total >= lo) & (total <= hi); owner = key & (N - 1); bucket = (key >> LN) & (Q - 1)
        for p in range(N):
            for g in range(8):
                got = [np.flatnonzero(alive[q, g] & (owner[q, g] == p))[:CAP] for q in range(N)]
                c = np.concatenate([k[q, g][:, got[q]] for q in range(N)], axis=1); bu = np.concatenate([bucket[q, g, got[q]] for q in range(N)])
                first = np.sort(np.unique(bu, return_index=True)[1])
                keep = first[free[p, g, bu[first]]]; e = int(tot[p, g])
                v[p, g][:, e:e + len(keep)] = c[:, keep]; free[p, g, bu[keep]] = False; n[p, g, s] = len(keep)
    return {"y": np.ascontiguousarray(v[..., B:]).reshape(N, 128, RO * M).astype(np.float32).astype(BF)}

@@ -1,0 +1,563 @@
+from concourse.bass import DstId, RemoteDMATransfer
+from concourse.mybir import AluOpType as A, ActivationFunctionType as F
+
+F32, BF, I32, U16 = "float32", "bfloat16", "int32", "uint16"
+B, J, CAP, N = 3072, 4096, 96, 4
+M = N * CAP
+MAGIC = 12582912.0
+HALF = -2047.5 / 4096
+MID = 1728
+BIAS = HALF - MID
+DEAD = 524288
+PAIR = 272
+INV = 1048576
+
+SCRATCH = {}
+ALIAS, COLS, SIZE = {}, {}, {F32: 0, BF: 0, I32: 0}
+for _n, _c, _d in [
+    ("nl", 8, I32), ("nf", 8, F32), ("sc", 8, F32), ("nq", 8, F32), ("cs4", 8, F32), ("ub", 8, F32), ("pr", 4, F32), ("wq", 4, F32), ("w", 4, F32),
+    ("one8", 128, F32), ("b8a", 128, F32), ("b8", 128, F32), ("on4", 8, F32),
+    ("pid", 1, I32), ("ri", 1, I32), ("rf", 1, F32), ("wk", 1, F32), ("wl0", 1, F32), ("wl", 1, F32), ("ur", 1, F32),
+    ("jc0", 256, F32), ("jc", 256, F32), ("trx0", 64, F32), ("trx", 64, F32), ("tk0", 24, F32), ("tk", 24, F32), ("tb0", 24, F32), ("tb", 24, F32),
+    ("ob", 128, BF), ("ba", 128, BF), ("blk", 128, BF), ("nb", 128, BF), ("nblk", 128, BF), ("tri", 128, BF), ("neg", 128, BF), ("stri", 128, BF),
+    ("kib", 128, BF), ("idn", 128, BF), ("kblk", 128, BF), ("mob", 128, BF), ("idp", 128, BF), ("idm", 128, BF),
+    ("onx", 2048, BF), ("kwx", 2048, BF), ("lwx", 2048, BF), ("tx", 2048, BF),
+    ("vd", 1024, BF), ("rst", 64, BF), ("one", 384, BF), ("p6", 64, BF), ("cap", 64, F32), ("p272", 24, BF), ("mone", 24, BF), ("ud", 384, I32),
+    ("mid", 1, F32), ("nmid", 1, F32), ("hl0", 1, F32), ("hlf", 1, F32),
+    ("bx0", 4, F32), ("by0", 4, F32), ("bx1", 4, F32), ("by1", 4, F32), ("wa", 1, F32), ("wb", 1, F32), ("k1", 1, F32),
+    ("scx0", 1, F32), ("scy0", 1, F32), ("scx1", 1, F32), ("scy1", 1, F32),
+    ("n4", 1, F32), ("n4q", 1, F32), ("tq", 1, F32), ("wx", 1, F32), ("w0", 1, F32), ("bia", 1, F32), ("b4", 1, F32),
+    ("la", 512, I32), ("lb", 512, I32), ("lc", 512, I32), ("laf", 512, F32), ("lbf", 512, F32), ("lcf", 512, F32),
+    ("ux0", 1024, F32), ("uy0", 1024, F32), ("ux1", 1280, F32), ("uy1", 1280, F32),
+    ("hx0", 1024, BF), ("hy0", 1024, BF), ("hx1", 1280, BF), ("hy1", 1280, BF), ("sox", 1280, F32), ("soy", 1280, F32),
+    ("zf", 256, F32), ("lx", 256, U16), ("ly", 256, U16), ("lz", 256, U16),
+    ("bk", B + 4 * M, BF), ("yv", J, BF), ("xv", 1024, BF), ("fv", J, BF), ("cand", J + 16, BF),
+    ("ab", 256, F32), ("dead", 256, F32), ("zt", 256, I32), ("z2", 256, I32), ("zb", 256, BF), ("ind", 1024, BF),
+    ("clb", 64, BF), ("csb", 64, BF), ("e0", 64, BF), ("iv", 64, F32), ("t1", 64, F32), ("t2", 64, F32), ("t3", 64, F32), ("off", 64, U16),
+    ("win0", 384 + 1024, BF), ("win1", 384 + 1024, BF), ("ns", 384, BF), ("c1", 384, BF), ("cnt", 384, BF), ("po", 24, U16), ("pref", 4 * PAIR, BF),
+    ("ll", 384, BF), ("jl", 24, U16), ("snd0", 288, BF), ("snd1", 288, BF), ("arr0", M, BF), ("arr1", M, BF),
+    ("ki", 24, I32), ("kb", 24, I32), ("kf", 24, F32), ("kb2", 24, I32), ("bm", 24, F32), ("bo", 24, U16), ("r32", M, I32), ("r33", M, I32), ("r16", M, U16),
+    ("tbl", J + 16 + M, I32), ("us", M, BF), ("eq", 24 * M, BF), ("dm", M, BF),
+    ("nk", 24, BF), ("kp", 24, BF), ("ks", 24, BF), ("tn", 24, F32), ("om", 24, F32), ("mo", 24, U16), ("tn2", 24, F32), ("om2", 24, F32), ("mo2", 24, U16),
+]:
+    COLS[_n] = _c
+    if _c <= 128 and _d != U16 and _n != "nl":
+        ALIAS[_n] = ({F32: "pf", BF: "pb", I32: "pi"}[_d], SIZE[_d])
+        SIZE[_d] += -(-_c // 8) * 8
+    else:
+        SCRATCH[_n] = ("sbuf", [128, _c], _d)
+SCRATCH["pf"] = ("sbuf", [128, SIZE[F32]], F32)
+SCRATCH["pb"] = ("sbuf", [128, SIZE[BF]], BF)
+SCRATCH["pi"] = ("sbuf", [128, SIZE[I32]], I32)
+for _n in range(8):
+    SCRATCH["ps%d" % _n] = ("psum", [128, 512], F32)
+
+DMAS = ["d_ncl", "d_lim", "d_la0", "d_lb0", "d_lc0", "d_la1", "d_lb1", "d_lc1", "d_bk", "d_used", "d_y"]
+SEMAPHORES = ["cv", "cs", "ct", "cg", "arrv0", "arrv1", "snt0", "snt1"] + DMAS
+
+
+def plan(src, cores, topo):
+    own = topo.cores_of(src)
+    far = [c for c in cores if c not in own]
+    out = {}
+    taken = []
+    for i, d in enumerate(far):
+        e = topo.engines(src, d)
+        n = len(e) // len(far)
+        out[d] = e[i * n:(i + 1) * n]
+        taken += e
+    for d in cores:
+        if d in own and d != src:
+            out[d] = [e for e in topo.engines(src, d) if e not in taken][:4]
+    return out
+
+
+def overlap(a, b):
+    if a.start >= b.stop or b.start >= a.stop:
+        return False
+    if a.step == b.step and a.step > 1 and (a.start - b.start) % a.step:
+        return False
+    return True
+
+
+def covers(a, b):
+    return a.step == 1 and a.start <= b.start and b.stop <= a.stop
+
+
+def rank_program(g, core, T, topo):
+    rank = T.rank_of(core)
+    if rank is None:
+        return
+    cores = list(T.cores)
+    queues = {"v": g.vector, "s": g.scalar, "t": g.tensor, "g": g, "y": g.sync}
+    qsem = {"v": "cv", "s": "cs", "t": "ct", "g": "cg"}
+    count = {"v": 0, "s": 0, "t": 0, "g": 0}
+    known = {q: {} for q in queues}
+    wrote, read = {}, {}
+    order = [0]
+
+    def need(q, toks):
+        for t in sorted(toks, key=lambda t: -t["n"]):
+            if known[q].get(t["sem"], 0) < t["val"]:
+                queues[q].wait_ge(T.sem[t["sem"]], t["val"])
+                for k, v in t["snap"].items():
+                    if known[q].get(k, 0) < v:
+                        known[q][k] = v
+                known[q][t["sem"]] = max(known[q].get(t["sem"], 0), t["val"])
+
+    def prepare(q, outs, ins):
+        toks = []
+        for n, r in ins:
+            for r2, t in wrote.get(n, []):
+                if overlap(r, r2):
+                    toks.append(t)
+            if n.startswith("ps"):
+                toks += [t for r2, t in wrote.get(n, []) + read.get(n, []) if t["q"] != q]
+        for n, r in outs:
+            ps = n.startswith("ps")
+            for r2, t in wrote.get(n, []):
+                if ps and t["q"] != q or (overlap(r, r2) and not (ps and q == "t")):
+                    toks.append(t)
+            for r2, t in read.get(n, []):
+                if t["q"] != q and (ps or overlap(r, r2)):
+                    toks.append(t)
+        need(q, toks)
+
+    def record(q, outs, ins, sem, val):
+        order[0] += 1
+        tok = {"n": order[0], "sem": sem, "val": val, "q": q, "snap": dict(known[q])}
+        for n, r in outs:
+            wrote[n] = [x for x in wrote.get(n, []) if not covers(r, x[0]) or n.startswith("ps")] + [(r, tok)]
+            if not n.startswith("ps"):
+                read[n] = [x for x in read.get(n, []) if not covers(r, x[0])]
+        for n, r in ins:
+            read[n] = [x for x in read.get(n, []) if not (x[1]["q"] == q and x[0] == r)] + [(r, tok)]
+        for n, r in outs + ins:
+            if n.startswith("ps"):
+                for d in (wrote, read):
+                    d[n] = list({(x[1]["q"], x[0].start, x[0].stop): x for x in d.get(n, [])}.values())
+
+    def R(name, a=0, b=None, st=1, rows=None):
+        b = COLS.get(name, 512) if b is None else b
+        if name in ALIAS:
+            name, o = ALIAS[name]
+            a, b = a + o, b + o
+        cols = slice(a, b) if st == 1 else slice(a, b, st)
+        ap = T[name][:, cols] if rows is None else T[name][rows, cols]
+        return (ap, [(name, range(a, b, st))])
+
+    def X(w, o):
+        return (w[0].indirect(o[0]), w[1] + o[1])
+
+    def emit(q, outs, ins, f):
+        prepare(q, outs, ins)
+        inst = f(queues[q])
+        count[q] += 1
+        inst.then_inc(T.sem[qsem[q]], 1)
+        record(q, outs, ins, qsem[q], count[q])
+
+    def scal(x):
+        return (x[0], x[1]) if isinstance(x, tuple) else (x, [])
+
+    def ts(o, i, s1, s2, op0, op1=None):
+        a, ra_ = scal(s1)
+        b, rb_ = scal(s2)
+        if op1 is None:
+            emit("v", o[1], i[1] + ra_, lambda e: e.tensor_scalar(o[0], i[0], a, None, op0))
+        else:
+            emit("v", o[1], i[1] + ra_ + rb_, lambda e: e.tensor_scalar(o[0], i[0], a, b, op0, op1))
+
+    def tt(o, a, b, op):
+        emit("v", o[1], a[1] + b[1], lambda e: e.tensor_tensor(o[0], a[0], b[0], op))
+
+    def cp(o, i):
+        emit("v", o[1], i[1], lambda e: e.tensor_copy(o[0], i[0]))
+
+    def scatter(w, o, i):
+        emit("v", w[1], i[1] + o[1], lambda e: e.tensor_copy(w[0].indirect(o[0]), i[0]))
+
+    def scan(o, a, b, op0, op1):
+        emit("v", o[1], a[1] + b[1], lambda e: e.tensor_tensor_scan(o[0], a[0], b[0], 0.0, op0, op1))
+
+    def fill(o, c):
+        emit("v", o[1], [], lambda e: e.memset(o[0], c))
+
+    def act(o, i, func, scale=None, bias=None):
+        kw, more = {}, []
+        for k, x in (("scale", scale), ("bias", bias)):
+            if x is not None:
+                kw[k] = x[0]
+                more = more + x[1]
+        emit("s", o[1], i[1] + more, lambda e: e.activation(o[0], i[0], func, **kw))
+
+    def mm(o, l, r, start, stop):
+        emit("t", o[1], l[1] + r[1], lambda e: e.matmul(o[0], l[0], r[0], start, stop))
+
+    def iota(o, pattern, base, cm=0):
+        emit("g", o[1], [], lambda e: e.iota(o[0], pattern, base, cm, allow_small_or_imprecise_dtypes=True))
+
+    def sel(o, i, pattern, op, base, cm):
+        emit("g", o[1], i[1], lambda e: e.affine_select(o[0], i[0], pattern, op, 0.0, base, cm))
+
+    def dma(q, sem, o, i):
+        prepare(q, o[1], i[1])
+        queues[q].dma_start(o[0], i[0]).then_inc(T.sem[sem], 16)
+        record(q, o[1], i[1], sem, 16)
+
+    def ext(ap):
+        return (ap, [])
+
+    def listify(o, wname, src, ncols, start, stop, st=16):
+        for x in range(16):
+            mm(o, R(wname, 128 * x, 128 * x + 128), R(src, x, ncols, st), start and x == 0, stop and x == 15)
+
+    def P(k, a, b):
+        return R("ps%d" % k, a, b)
+
+    def spread(name, src):
+        for x in range(16):
+            act(R(name, 129 * x, 128 * x + 128, 16), R(src, x, 128, 16), F.Copy)
+
+    first8 = slice(0, 8)
+    dma("y", "d_ncl", R("nl", 0, 4, rows=first8), ext(T.ncl[:, :]))
+    dma("s", "d_lim", R("nl", 4, 6, rows=first8), ext(T.lim[:, :]))
+    dma("y", "d_lb0", R("lb", 0, 256), ext(T.rb[:, 0:256]))
+    dma("s", "d_la0", R("la", 0, 256), ext(T.ra[:, 0:256]))
+    dma("y", "d_lc0", R("lc", 0, 256), ext(T.rc[:, 0:256]))
+    dma("y", "d_bk", R("bk", 0, B), ext(T.bank[:, :]))
+    dma("y", "d_lb1", R("lb", 256, 512), ext(T.rb[:, 256:512]))
+    dma("y", "d_la1", R("la", 256, 512), ext(T.ra[:, 256:512]))
+    dma("y", "d_lc1", R("lc", 256, 512), ext(T.rc[:, 256:512]))
+
+    fill(R("ob"), 1.0)
+    fill(R("one8"), 1.0)
+    fill(R("onx"), 0.0)
+    sel(R("ba"), R("ob"), [[-16, 8], [0, 16]], A.is_ge, 0, 1)
+    sel(R("blk"), R("ba"), [[16, 8], [0, 16]], A.is_ge, 15, -1)
+    iota(R("pid"), [[0, 1]], 0, 1)
+    sel(R("b8a", rows=first8), R("one8", rows=first8), [[1, 128]], A.is_ge, 0, -16)
+    sel(R("b8", rows=first8), R("b8a", rows=first8), [[-1, 128]], A.is_ge, 15, 16)
+    iota(R("jc0"), [[16, 256]], -2048)
+    for h in ("hy0", "hx0"):
+        iota(R(h, 0, 1024, 4), [[0, 256]], -4096)
+    fill(R("on4"), 1.0)
+    fill(R("ub", 0, 1), BIAS)
+    fill(R("bia"), BIAS)
+    fill(R("b4"), B + BIAS)
+    fill(R("by0", 1, 2), -2048.0)
+    ts(R("ri"), R("pid"), 15, None, A.bitwise_and)
+    cp(R("rf"), R("ri"))
+    ts(R("wk"), R("rf"), 14.0, 9.0, A.mult, A.add)
+    ts(R("wl0"), R("rf"), 15.0, 8191.0, A.is_equal, A.mult)
+    ts(R("wl"), R("wl0"), 1.0, None, A.add)
+    ts(R("jc"), R("jc0"), R("rf"), None, A.add)
+    spread("onx", "blk")
+    act(R("kwx"), R("onx"), F.Copy, scale=R("wk"))
+
+    cp(R("nf", 0, 6, rows=first8), R("nl", 0, 6, rows=first8))
+    mm(P(7, 0, 6), R("b8", rows=first8), R("nf", 0, 6, rows=first8), True, True)
+    cp(R("sc", 0, 6), P(7, 0, 6))
+    for k, (a, b) in enumerate(((0, 3), (1, 2), (1, 3), (2, 2))):
+        tt(R("pr", k, k + 1), R("sc", a, a + 1), R("sc", b, b + 1), A.mult)
+    scan(R("cs4", 0, 4), R("on4", 0, 4), R("sc", 0, 4), A.mult, A.add)
+    ts(R("wq"), R("pr"), 1.0 / 4096, HALF, A.mult, A.add)
+    ts(R("nq", 0, 4), R("sc", 0, 4), 1.0 / 4096, None, A.mult)
+    ts(R("w"), R("wq"), MAGIC, MAGIC, A.add, A.subtract)
+    ts(R("ub", 1, 4), R("cs4", 0, 3), BIAS, None, A.add)
+    tt(R("wa"), R("w", 0, 1), R("w", 1, 2), A.add)
+    ts(R("by0", 0, 1), R("w", 1, 2), -16777216.0, -2048.0, A.mult, A.add)
+    ts(R("by0", 2, 3), R("w", 1, 2), 16777216.0, -2048.0, A.mult, A.add)
+    ts(R("scy0"), R("wa"), -8192.0, None, A.mult)
+    ts(R("scx0"), R("wa"), 8192.0, None, A.mult)
+    ts(R("bx0", 0, 3), R("by0", 0, 3), -1.0, None, A.mult)
+
+    def affine(t, who, k, s):
+        i = s - 1 - k
+        act(R("u%s%d" % (who, t), i, 256 * s, s), R("l%sf" % ("a" if who == "x" else "b"), 256 * t, 256 * t + 256), F.Identity,
+            scale=R("nq", k, k + 1), bias=R("ub", k, k + 1))
+
+    def hmask(t, who, i, s):
+        k = s - 1 - i if who == "x" else i - 1
+        act(R("h%s%d" % (who, t), i, 256 * s, s), R("jc"), F.Identity, scale=R("sc%s%d" % (who, t)), bias=R("b%s%d" % (who, t), k, k + 1))
+
+    def places(t, who, s):
+        o = "so" + who
+        scan(R(o, 0, 256 * s), R("h%s%d" % (who, t)), R("u%s%d" % (who, t)), A.min, A.max)
+        ts(R("l" + who), R(o, s - 1, 256 * s, s), MAGIC, MAGIC - MID, A.add, A.subtract)
+
+    def gather_y(q, wid):
+        act(R("yv", 1024 * q, 1024 * q + 1024), X(R("bk", 0, wid), R("ly", 64 * q, 64 * q + 64)), F.Copy)
+
+    def first(q, wid):
+        tt(R("fv", 1024 * q, 1024 * q + 1024), X(R("bk", 0, wid), R("lx", 64 * q, 64 * q + 64)), R("yv", 1024 * q, 1024 * q + 1024),
+           (A.min, A.max, None, A.add)[q])
+
+    def third(q, wid):
+        tt(R("cand", 1024 * q, 1024 * q + 1024), X(R("bk", 0, wid), R("lz", 64 * q, 64 * q + 64)), R("fv", 1024 * q, 1024 * q + 1024), A.min)
+
+    def sums(q):
+        o = (0, 64 * q, 192 + 64 * q) if q < 3 else (1, 0, 64)
+        for w, c in (("onx", o[1]), ("kwx", o[2])):
+            for x in range(16):
+                mm(P(o[0], c, c + 64), R(w, 128 * x, 128 * x + 128), R("cand", 1024 * q + x, 1024 * q + 1024, 16), x == 0, x == 15)
+
+    owners = [(rank + 1 + i) % N for i in range(N)]
+
+    def classify(k, c, n, cs, ck):
+        act(R("ab", c, c + n), P(k, cs, cs + n), F.Abs, bias=R("nmid"))
+        ts(R("dead", c, c + n), R("ab", c, c + n), R("hlf"), float(DEAD), A.is_gt, A.mult)
+        tt(R("zt", c, c + n), R("dead", c, c + n), P(k, ck, ck + n), A.add)
+        ts(R("z2", c, c + n), R("zt", c, c + n), DEAD + 3, None, A.bitwise_and)
+        z = "z2"
+        if n > 64:
+            z = "zb"
+            cp(R("zb", c, c + n), R("z2", c, c + n))
+        for i, p in enumerate(owners):
+            ts(R("ind", 256 * i + c, 256 * i + c + n), R(z, c, c + n), float(p), None, A.is_equal)
+
+    def build(t, wid, later):
+        for q in (0, 1, 2):
+            gather_y(q, wid)
+        act(R("xv"), X(R("bk", 0, wid), R("lx", 128, 192)), F.Copy)
+        first(0, wid)
+        gather_y(3, wid)
+        third(0, wid)
+        sums(0)
+        for h in range(2):
+            mm(P(2 + h, 0, 512), R("idp"), R("xv", 512 * h, 512 * h + 512), True, False)
+            mm(P(2 + h, 0, 512), R("idm"), R("yv", 2048 + 512 * h, 2560 + 512 * h), False, True)
+            act(R("fv", 2048 + 512 * h, 2560 + 512 * h), P(2 + h, 0, 512), F.Abs)
+        later()
+        first(1, wid)
+        third(1, wid)
+        sums(1)
+        first(3, wid)
+        third(2, wid)
+        sums(2)
+        third(3, wid)
+        sums(3)
+        classify(0, 0, 192, 0, 192)
+        classify(1, 192, 64, 0, 64)
+
+    def send(t, gap1, gap2, gap3):
+        win, arr, snd = "win%d" % t, "arr%d" % t, "snd%d" % t
+        listify(P(4, 0, 64), "onx", "ind", 1024, True, True)
+        gap1()
+        cp(R("clb"), P(4, 0, 64))
+        scan(R("csb"), R("rst"), R("clb"), A.mult, A.add)
+        ts(R("e0"), R("clb"), 0.0, None, A.is_equal)
+        mm(P(5, 0, 64), R("blk"), R("p6"), True, False)
+        mm(P(5, 0, 64), R("neg"), R("clb"), False, False)
+        mm(P(5, 0, 64), R("blk"), R("csb"), False, False)
+        mm(P(5, 0, 64), R("idn"), R("e0"), False, True)
+        tt(R("iv"), P(5, 0, 64), R("cap"), A.is_ge)
+        ts(R("t2"), P(5, 0, 64), 383.0, None, A.min)
+        tt(R("t1"), R("iv"), R("trx"), A.mult)
+        tt(R("t3"), R("t1"), R("t2"), A.max)
+        cp(R("off"), R("t3"))
+        for h in range(2):
+            mm(P(2 + h, 0, 512), R("tri"), R("ind", 512 * h, 512 * h + 512), True, True)
+        for i in range(4):
+            act(R("pref", PAIR * i + 1, PAIR * i + 257), P(2 + i // 2, 256 * (i % 2), 256 * (i % 2) + 256), F.Copy)
+        scatter(R(win), R("off"), R("vd"))
+        ts(R("ns"), R(win, 0, 384), 0.0, None, A.is_equal)
+        scan(R("c1"), R("ns"), R(win, 0, 384), A.mult, A.add)
+        mm(P(5, 64, 88), R("blk"), R("p272"), True, False)
+        listify(P(5, 64, 88), "onx", "c1", 384, False, True)
+        scan(R("cnt"), R("ns"), R("one"), A.mult, A.add)
+        gap2()
+        ts(R("po"), P(5, 64, 88), 1.0 / 16, None, A.mult)
+        mm(P(6, 0, 24), R("blk"), R("mone"), True, False)
+        listify(P(6, 0, 24), "onx", "c1", 384, False, False)
+        tt(R("ll"), X(R("pref"), R("po")), R("cnt"), A.is_lt)
+        gap3()
+        listify(P(6, 0, 24), "lwx", "ll", 384, False, True)
+        ts(R("jl"), P(6, 0, 24), float(J), None, A.min)
+        cp(R(snd), X(R("cand"), R("jl", 0, 18)))
+        mine = plan(core, cores, topo)
+        src = [R(snd, CAP * i, CAP * i + CAP) for i in range(N - 1)]
+        prepare("g", [], [x for s in src for x in s[1]])
+        tr = []
+        for i in range(N - 1):
+            d = cores[owners[i]]
+            rid, pid = topo.addr(d, core)
+            tr.append(RemoteDMATransfer(dst_ids=[DstId(rid=rid, pnc=pid)], dma_engine_mask=sum(1 << e for e in mine[d]),
+                                        remote_sem=T.sem["arrv%d" % t], src=src[i][0], dst=T[arr][:, CAP * rank:CAP * rank + CAP]))
+        g.remote_dma_fused(tr, local_sem=T.sem["snt%d" % t])
+        cp(R(arr, CAP * rank, CAP * rank + CAP), X(R("cand"), R("jl", 18, 24)))
+        total = sum(len(plan(c, cores, topo)[core]) for c in cores if c != core)
+        order[0] += 1
+        tok = {"n": order[0], "sem": "arrv%d" % t, "val": total, "q": "r", "snap": {}}
+        for q in range(N):
+            if q != rank:
+                wrote.setdefault(arr, []).append((range(CAP * q, CAP * q + CAP), tok))
+        return sum(len(e) for e in mine.values()), total
+
+    def keep(t, base):
+        arr = "arr%d" % t
+        mm(P(2, 0, M), R("kblk"), R(arr), True, True)
+        listify(P(3, 0, 24), "kwx", arr, M, True, True)
+        cp(R("r32"), P(2, 0, M))
+        ts(R("r33"), R("r32"), INV + 16383, None, A.bitwise_and)
+        cp(R("ki"), P(3, 0, 24))
+        cp(R("r16"), R("r33"))
+        ts(R("kb"), R("ki"), INV + 16383, None, A.bitwise_and)
+        ts(R("kb2"), R("kb"), 2, None, A.arith_shift_right)
+        cp(R("kf"), R("kb"))
+        ts(R("bo"), R("kb2"), J, None, A.min)
+        cp(R("us"), X(R("tbl", 0, J + 16), R("bo")))
+        mm(P(0, 0, M), R("blk"), R("us"), True, False)
+        for q in range(24):
+            ts(R("eq", 400 * q, M * q + M), R("r16", 16 * q, M), R("kf", q, q + 1), None, A.is_equal)
+            if q < 23:
+                mm(P(0, 16 * q + 16, M), R("blk"), R("eq", 400 * q + 16, M * q + M), False, q == 22)
+        listify(P(1, 0, 24), "tx", "eq", 24 * M, True, False, 400)
+        cp(R("dm"), P(0, 0, M))
+        listify(P(1, 0, 24), "onx", "dm", M, False, True)
+        ts(R("kp"), P(1, 0, 24), 0.0, None, A.is_equal)
+        ts(R("nk"), P(1, 0, 24), 0.0, None, A.is_gt)
+        scan(R("ks"), R("one", 0, 24), R("kp"), A.mult, A.add)
+        tt(R("tn"), R("nk"), R("tk"), A.mult)
+        if t == 0:
+            mm(P(7, 8, 9), R("blk"), R("ks", 23, 24), True, True)
+        mm(P(4, 64, 88), R("neg"), R("kp"), True, False)
+        mm(P(4, 64, 88), R("blk"), R("ks"), False, True)
+        if t == 0:
+            cp(R("n4"), P(7, 8, 9))
+            ts(R("wx"), R("n4"), R("nq", 0, 1), HALF, A.mult, A.add)
+            ts(R("w0"), R("wx"), MAGIC, MAGIC, A.add, A.subtract)
+            ts(R("scy1"), R("w0"), -8192.0, R("k1"), A.mult, A.subtract)
+            ts(R("scx1"), R("w0"), 8192.0, R("k1"), A.mult, A.add)
+            ts(R("n4q"), R("n4"), 1.0 / 4096, None, A.mult)
+            ts(R("tq"), R("n4"), 1.0 / 4096, B / 4096.0, A.mult, A.add)
+        tt(R("om"), R("tn"), P(4, 64, 88), A.max)
+        if base is None:
+            cp(R("mo"), R("om"))
+        else:
+            ts(R("mo"), R("om"), base, None, A.add)
+
+    def append(t):
+        scatter(R("bk", B, B + 4 * M), R("mo"), R("arr%d" % t))
+
+    for i in range(1, 4):
+        hmask(0, "y", i, 4)
+    for i in range(1, 4):
+        hmask(0, "x", i, 4)
+    cp(R("laf", 0, 256), R("la", 0, 256))
+    for k in range(4):
+        affine(0, "x", k, 4)
+    for k in range(4):
+        ts(R("uy0", 3 - k, 1024, 4), R("lb", 0, 256), R("nq", k, k + 1), R("ub", k, k + 1), A.mult, A.add)
+    places(0, "y", 4)
+    places(0, "x", 4)
+    ts(R("zf"), R("lc", 0, 256), B / 4096.0, BIAS, A.mult, A.add)
+    ts(R("lz"), R("zf"), MAGIC, MAGIC - MID, A.add, A.subtract)
+    iota(R("mob"), [[0, 128]], -1)
+    iota(R("kib"), [[0, 128]], 1024)
+    sel(R("idp"), R("ob"), [[-1, 128]], A.is_equal, 0, 1)
+    sel(R("idm"), R("mob"), [[-1, 128]], A.is_equal, 0, 1)
+    sel(R("nb"), R("mob"), [[-16, 8], [0, 16]], A.is_ge, 0, 1)
+    sel(R("nblk"), R("nb"), [[16, 8], [0, 16]], A.is_ge, 15, -1)
+    sel(R("neg"), R("nblk"), [[-1, 128]], A.is_ge, 0, 1)
+    sel(R("tri"), R("blk"), [[1, 128]], A.is_ge, 0, -1)
+    sel(R("idn"), R("kib"), [[-1, 128]], A.is_equal, 0, 1)
+    iota(R("cand", J, J + 16), [[0, 16]], -1)
+    iota(R("trx0"), [[16, 64]], 384)
+    iota(R("rst"), [[0, 64]], 1)
+    iota(R("cap"), [[CAP, 4], [0, 16]], CAP)
+    iota(R("p6"), [[6, 4], [0, 16]], 0)
+    iota(R("rst", 0, 64, 16), [[0, 4]], 0)
+    iota(R("win0", 0, 384), [[0, 384]], 0)
+    iota(R("vd"), [[0, 4], [1, 256]], 1)
+    iota(R("win0", 0, 384, CAP), [[0, 4]], -1)
+    iota(R("pref"), [[0, 4 * PAIR]], 0)
+    iota(R("p272"), [[PAIR, 4], [0, 6]], 0)
+    iota(R("one"), [[0, 384]], 1)
+    iota(R("mone"), [[0, 24]], -1)
+    iota(R("tk0"), [[16, 24]], 2 * M)
+    iota(R("tb0"), [[16, 24]], J + 16)
+    sel(R("stri"), R("blk"), [[1, 128]], A.is_ge, -1, -1)
+    iota(R("tbl"), [[0, J + 16 + M]], 0)
+    iota(R("tx"), [[0, 2048]], 0)
+    iota(R("bk", B, B + 4 * M), [[0, 4 * M]], 0)
+    for h in ("hy1", "hx1"):
+        iota(R(h, 0, 1280, 5), [[0, 256]], -4096)
+    tt(R("mid"), R("sc", 4, 5), R("sc", 5, 6), A.add)
+    tt(R("hl0"), R("sc", 5, 6), R("sc", 4, 5), A.subtract)
+    ts(R("nmid"), R("mid"), -0.5, None, A.mult)
+    ts(R("hlf"), R("hl0"), 0.5, None, A.mult)
+
+    build(0, B, lambda: act(R("lwx"), R("onx"), F.Copy, scale=R("wl")))
+
+    def gap0a():
+        ts(R("trx"), R("trx0"), R("rf"), None, A.add)
+        ts(R("tk"), R("tk0"), R("rf"), None, A.add)
+        ts(R("kblk"), R("blk"), R("wk"), None, A.mult)
+
+    def gap0b():
+        cp(R("lbf", 256, 512), R("lb", 256, 512))
+        fill(R("tbl", J, J + 16), 1)
+        for k in range(4):
+            affine(1, "y", k, 5)
+
+    def gap0c():
+        cp(R("laf", 256, 512), R("la", 256, 512))
+        cp(R("lcf", 256, 512), R("lc", 256, 512))
+        for k in range(4):
+            affine(1, "x", k, 5)
+
+    sent0, got0 = send(0, gap0a, gap0b, gap0c)
+
+    dma("y", "d_used", R("tbl", 0, J, rows=slice(0, 128, 16)), ext(T.used[:, :]))
+    spread("tx", "stri")
+    for i in range(2):
+        iota(R("win1", 0, 384, CAP if i else 1), [[0, 4 if i else 384]], -i)
+    ts(R("wb"), R("w", 2, 3), 2.0, R("w", 3, 4), A.mult, A.add)
+    ts(R("by1", 1, 2), R("w", 3, 4), -8388608.0, -2048.0, A.mult, A.add)
+    ts(R("by1", 2, 3), R("w", 3, 4), 8388608.0, -2048.0, A.mult, A.add)
+    ts(R("k1"), R("wb"), 4096.0, None, A.mult)
+    ts(R("by1", 0, 1), R("wb"), -8388608.0, -2048.0, A.mult, A.add)
+    ts(R("by1", 3, 4), R("wb"), 8388608.0, -2048.0, A.mult, A.add)
+    ts(R("ur"), R("rf"), 0.0, None, A.is_equal)
+    ts(R("bx1"), R("by1"), -1.0, None, A.mult)
+
+    keep(0, None)
+
+    for i in range(1, 5):
+        hmask(1, "y", i, 5)
+    act(R("ux1", 0, 1280, 5), R("laf", 256, 512), F.Identity, scale=R("n4q"), bias=R("b4"))
+    act(R("zf"), R("lcf", 256, 512), F.Identity, scale=R("tq"), bias=R("bia"))
+    for i in range(1, 5):
+        hmask(1, "x", i, 5)
+    append(0)
+    ts(R("uy1", 0, 1280, 5), R("lb", 256, 512), R("n4q"), B + BIAS, A.mult, A.add)
+    places(1, "y", 5)
+    places(1, "x", 5)
+    ts(R("lz"), R("zf"), MAGIC, MAGIC - MID, A.add, A.subtract)
+    build(1, B + M, lambda: None)
+
+    def gap1a():
+        ts(R("ud"), R("one"), R("ur"), None, A.mult)
+        ts(R("tb"), R("tb0"), R("rf"), None, A.add)
+
+    def gap1b():
+        ts(R("bm"), R("kb2"), float(J), None, A.min)
+        tt(R("tn2"), R("nk"), R("tb"), A.mult)
+        tt(R("om2"), R("tn2"), R("bm"), A.max)
+        cp(R("mo2"), R("om2"))
+
+    sent1, got1 = send(1, gap1a, gap1b, lambda: None)
+    scatter(R("tbl"), R("mo2"), R("ud"))
+
+    keep(1, R("n4"))
+    append(1)
+    dma("y", "d_y", ext(T.y[:, :]), R("bk", B, B + 2 * M))
+
+    g.wait_ge(T.sem.snt0, sent0)
+    g.wait_ge(T.sem.snt1, sent1)
+    g.wait_ge(T.sem.arrv0, got0)
+    g.wait_ge(T.sem.arrv1, got1)
+    for d in DMAS:
+        g.wait_ge(T.sem[d], 16)
+    for q in qsem:
+        g.wait_ge(T.sem[qsem[q]], count[q])

@@ -11,30 +11,32 @@ BIAS = HALF - MID
 DEAD = 524288
 PAIR = 272
 INV = 1048576
+UNIT = 32
 
 SCRATCH = {}
 ALIAS, COLS, SIZE = {}, {}, {F32: 0, BF: 0, I32: 0}
 for _n, _c, _d in [
     ("nl", 8, I32), ("nf", 8, F32), ("sc", 8, F32), ("nq", 8, F32), ("cs4", 8, F32), ("ub", 8, F32), ("pr", 4, F32), ("wq", 4, F32), ("w", 4, F32),
     ("one8", 128, F32), ("b8a", 128, F32), ("b8", 128, F32), ("on4", 8, F32),
-    ("pid", 1, I32), ("ri", 1, I32), ("rf", 1, F32), ("wk", 1, F32), ("wl0", 1, F32), ("wl", 1, F32), ("ur", 1, F32),
-    ("jc0", 256, F32), ("jc", 256, F32), ("trx0", 64, F32), ("trx", 64, F32), ("tk0", 24, F32), ("tk", 24, F32), ("tb0", 24, F32), ("tb", 24, F32),
+    ("pid", 1, I32), ("ri", 1, I32), ("rf", 1, F32), ("wk", 1, F32), ("wl0", 1, F32), ("wl", 1, F32),
+    ("jc0", 256, F32), ("jc", 256, F32), ("trx0", 64, F32), ("tk0", 24, F32), ("tk", 24, F32), ("tb0", 24, F32), ("tb", 24, F32),
     ("ob", 128, BF), ("ba", 128, BF), ("blk", 128, BF), ("nb", 128, BF), ("nblk", 128, BF), ("tri", 128, BF), ("neg", 128, BF), ("stri", 128, BF),
-    ("kib", 128, BF), ("idn", 128, BF), ("kblk", 128, BF), ("mob", 128, BF), ("idp", 128, BF), ("idm", 128, BF),
+    ("kib", 128, BF), ("idn", 128, BF), ("kblk", 128, BF), ("mob", 128, BF), ("idp", 128, BF), ("idm", 128, BF), ("z16", 16, BF),
     ("onx", 2048, BF), ("kwx", 2048, BF), ("lwx", 2048, BF), ("tx", 2048, BF),
-    ("vd", 1024, BF), ("rst", 64, BF), ("one", 384, BF), ("p6", 64, BF), ("cap", 64, F32), ("p272", 24, BF), ("mone", 24, BF), ("ud", 384, I32),
-    ("mid", 1, F32), ("nmid", 1, F32), ("hl0", 1, F32), ("hlf", 1, F32),
-    ("bx0", 4, F32), ("by0", 4, F32), ("bx1", 4, F32), ("by1", 4, F32), ("wa", 1, F32), ("wb", 1, F32), ("k1", 1, F32),
+    ("vd", 512, BF), ("vdb", 512, F32), ("rst", 64, BF), ("one", 384, BF), ("p6", 64, BF), ("cap", 64, F32), ("p272", 24, BF), ("mone", 24, BF), ("ud", 384, I32),
+    ("nmid", 1, F32), ("nhl", 1, F32), ("qd", 1, F32), ("q1", 1, F32), ("b75", 1, F32), ("bia", 1, F32), ("b4", 1, F32),
+    ("bx0", 4, F32), ("by0", 4, F32), ("bx1", 4, F32), ("by1", 4, F32), ("wb", 1, F32), ("k1", 1, F32),
     ("scx0", 1, F32), ("scy0", 1, F32), ("scx1", 1, F32), ("scy1", 1, F32),
-    ("n4", 1, F32), ("n4q", 1, F32), ("tq", 1, F32), ("wx", 1, F32), ("w0", 1, F32), ("bia", 1, F32), ("b4", 1, F32),
+    ("n4", 1, F32), ("n4q", 1, F32), ("tq", 1, F32), ("wx", 1, F32), ("w0", 1, F32),
     ("la", 512, I32), ("lb", 512, I32), ("lc", 512, I32), ("laf", 512, F32), ("lbf", 512, F32), ("lcf", 512, F32),
     ("ux0", 1024, F32), ("uy0", 1024, F32), ("ux1", 1280, F32), ("uy1", 1280, F32),
     ("hx0", 1024, BF), ("hy0", 1024, BF), ("hx1", 1280, BF), ("hy1", 1280, BF), ("sox", 1280, F32), ("soy", 1280, F32),
     ("zf", 256, F32), ("lx", 256, U16), ("ly", 256, U16), ("lz", 256, U16),
     ("bk", B + 4 * M, BF), ("yv", J, BF), ("xv", 1024, BF), ("fv", J, BF), ("cand", J + 16, BF),
     ("ab", 256, F32), ("dead", 256, F32), ("zt", 256, I32), ("z2", 256, I32), ("zb", 256, BF), ("ind", 1024, BF),
-    ("clb", 64, BF), ("csb", 64, BF), ("e0", 64, BF), ("iv", 64, F32), ("t1", 64, F32), ("t2", 64, F32), ("t3", 64, F32), ("off", 64, U16),
-    ("win0", 384 + 1024, BF), ("win1", 384 + 1024, BF), ("ns", 384, BF), ("c1", 384, BF), ("cnt", 384, BF), ("po", 24, U16), ("pref", 4 * PAIR, BF),
+    ("clb", 64, BF), ("csb", 64, BF), ("e0", 64, BF), ("iv", 64, F32), ("t1", 64, F32), ("t3", 64, F32), ("off", 64, U16),
+    ("win0", 704, BF), ("win1", 704, BF), ("wib0", 704, F32), ("wib1", 704, F32),
+    ("ns", 384, BF), ("c1", 384, BF), ("cnt", 384, BF), ("po", 24, U16), ("pref", 4 * PAIR, BF),
     ("ll", 384, BF), ("jl", 24, U16), ("snd0", 288, BF), ("snd1", 288, BF), ("arr0", M, BF), ("arr1", M, BF),
     ("ki", 24, I32), ("kb", 24, I32), ("kf", 24, F32), ("kb2", 24, I32), ("bm", 24, F32), ("bo", 24, U16), ("r32", M, I32), ("r33", M, I32), ("r16", M, U16),
     ("tbl", J + 16 + M, I32), ("us", M, BF), ("eq", 24 * M, BF), ("dm", M, BF),
@@ -199,10 +201,11 @@ def rank_program(g, core, T, topo):
     def sel(o, i, pattern, op, base, cm):
         emit("g", o[1], i[1], lambda e: e.affine_select(o[0], i[0], pattern, op, 0.0, base, cm))
 
-    def dma(q, sem, o, i):
-        prepare(q, o[1], i[1])
+    def dma(q, sem, o, i, total=16):
+        if total == 16:
+            prepare(q, o[1], i[1])
         queues[q].dma_start(o[0], i[0]).then_inc(T.sem[sem], 16)
-        record(q, o[1], i[1], sem, 16)
+        record(q, o[1], i[1], sem, total)
 
     def ext(ap):
         return (ap, [])
@@ -214,8 +217,8 @@ def rank_program(g, core, T, topo):
     def P(k, a, b):
         return R("ps%d" % k, a, b)
 
-    def spread(name, src):
-        for x in range(16):
+    def spread(name, src, xs=range(16)):
+        for x in xs:
             act(R(name, 129 * x, 128 * x + 128, 16), R(src, x, 128, 16), F.Copy)
 
     first8 = slice(0, 8)
@@ -228,47 +231,52 @@ def rank_program(g, core, T, topo):
     dma("y", "d_lb1", R("lb", 256, 512), ext(T.rb[:, 256:512]))
     dma("y", "d_la1", R("la", 256, 512), ext(T.ra[:, 256:512]))
     dma("y", "d_lc1", R("lc", 256, 512), ext(T.rc[:, 256:512]))
+    for r in range(16):
+        dma("y", "d_used", R("tbl", 0, J, rows=slice(r, 128, 16)), ext(T.used[:, :]), 256)
 
     fill(R("ob"), 1.0)
     fill(R("one8"), 1.0)
+    iota(R("pid"), [[0, 1]], 0, 1)
+    ts(R("ri"), R("pid"), 15, None, A.bitwise_and)
+    cp(R("rf"), R("ri"))
     fill(R("onx"), 0.0)
+    ts(R("wk"), R("rf"), 14.0, 9.0, A.mult, A.add)
+    ts(R("wl0"), R("rf"), 15.0, 8191.0 * UNIT, A.is_equal, A.mult)
     sel(R("ba"), R("ob"), [[-16, 8], [0, 16]], A.is_ge, 0, 1)
     sel(R("blk"), R("ba"), [[16, 8], [0, 16]], A.is_ge, 15, -1)
-    iota(R("pid"), [[0, 1]], 0, 1)
     sel(R("b8a", rows=first8), R("one8", rows=first8), [[1, 128]], A.is_ge, 0, -16)
     sel(R("b8", rows=first8), R("b8a", rows=first8), [[-1, 128]], A.is_ge, 15, 16)
     iota(R("jc0"), [[16, 256]], -2048)
     for h in ("hy0", "hx0"):
         iota(R(h, 0, 1024, 4), [[0, 256]], -4096)
-    fill(R("on4"), 1.0)
-    fill(R("ub", 0, 1), BIAS)
-    fill(R("bia"), BIAS)
-    fill(R("b4"), B + BIAS)
-    fill(R("by0", 1, 2), -2048.0)
-    ts(R("ri"), R("pid"), 15, None, A.bitwise_and)
-    cp(R("rf"), R("ri"))
-    ts(R("wk"), R("rf"), 14.0, 9.0, A.mult, A.add)
-    ts(R("wl0"), R("rf"), 15.0, 8191.0, A.is_equal, A.mult)
-    ts(R("wl"), R("wl0"), 1.0, None, A.add)
-    ts(R("jc"), R("jc0"), R("rf"), None, A.add)
-    spread("onx", "blk")
-    act(R("kwx"), R("onx"), F.Copy, scale=R("wk"))
+    spread("onx", "blk", range(10))
 
     cp(R("nf", 0, 6, rows=first8), R("nl", 0, 6, rows=first8))
     mm(P(7, 0, 6), R("b8", rows=first8), R("nf", 0, 6, rows=first8), True, True)
+    for x in range(10, 16):
+        cp(R("onx", 129 * x, 128 * x + 128, 16), R("blk", x, 128, 16))
+    act(R("kwx"), R("onx"), F.Copy, scale=R("wk"))
     cp(R("sc", 0, 6), P(7, 0, 6))
-    for k, (a, b) in enumerate(((0, 3), (1, 2), (1, 3), (2, 2))):
-        tt(R("pr", k, k + 1), R("sc", a, a + 1), R("sc", b, b + 1), A.mult)
-    scan(R("cs4", 0, 4), R("on4", 0, 4), R("sc", 0, 4), A.mult, A.add)
-    ts(R("wq"), R("pr"), 1.0 / 4096, HALF, A.mult, A.add)
-    ts(R("nq", 0, 4), R("sc", 0, 4), 1.0 / 4096, None, A.mult)
-    ts(R("w"), R("wq"), MAGIC, MAGIC, A.add, A.subtract)
-    ts(R("ub", 1, 4), R("cs4", 0, 3), BIAS, None, A.add)
-    tt(R("wa"), R("w", 0, 1), R("w", 1, 2), A.add)
+
+    def pairs(k, ab):
+        for i, (a, b) in enumerate(ab):
+            tt(R("pr", k + i, k + i + 1), R("sc", a, a + 1), R("sc", b, b + 1), A.mult)
+        ts(R("wq", k, k + 2), R("pr", k, k + 2), 1.0 / 4096, HALF, A.mult, A.add)
+
+    pairs(0, ((0, 3), (1, 2)))
+    ts(R("jc"), R("jc0"), R("rf"), None, A.add)
+    ts(R("w", 0, 2), R("wq", 0, 2), MAGIC, MAGIC, A.add, A.subtract)
+    fill(R("by0", 1, 2), -2048.0)
+    fill(R("on4"), 1.0)
     ts(R("by0", 0, 1), R("w", 1, 2), -16777216.0, -2048.0, A.mult, A.add)
     ts(R("by0", 2, 3), R("w", 1, 2), 16777216.0, -2048.0, A.mult, A.add)
-    ts(R("scy0"), R("wa"), -8192.0, None, A.mult)
-    ts(R("scx0"), R("wa"), 8192.0, None, A.mult)
+    ts(R("scy0"), R("w", 0, 1), R("w", 1, 2), -8192.0, A.add, A.mult)
+    ts(R("nq", 0, 4), R("sc", 0, 4), 1.0 / 4096, None, A.mult)
+    scan(R("cs4", 0, 4), R("on4", 0, 4), R("sc", 0, 4), A.mult, A.add)
+    fill(R("ub", 0, 1), BIAS)
+    ts(R("scx0"), R("w", 0, 1), R("w", 1, 2), 8192.0, A.add, A.mult)
+    ts(R("ub", 1, 4), R("cs4", 0, 3), BIAS, None, A.add)
+    ts(R("wl"), R("wl0"), float(UNIT), None, A.add)
     ts(R("bx0", 0, 3), R("by0", 0, 3), -1.0, None, A.mult)
 
     def affine(t, who, k, s):
@@ -296,26 +304,23 @@ def rank_program(g, core, T, topo):
         tt(R("cand", 1024 * q, 1024 * q + 1024), X(R("bk", 0, wid), R("lz", 64 * q, 64 * q + 64)), R("fv", 1024 * q, 1024 * q + 1024), A.min)
 
     def sums(q):
-        o = (0, 64 * q, 192 + 64 * q) if q < 3 else (1, 0, 64)
-        for w, c in (("onx", o[1]), ("kwx", o[2])):
+        o = ((0, 64 * q), (0, 128 + 64 * q)) if q < 2 else ((1, 64 * q - 128), (6, 64 * q))
+        for w, (k, c) in zip(("onx", "kwx"), o):
             for x in range(16):
-                mm(P(o[0], c, c + 64), R(w, 128 * x, 128 * x + 128), R("cand", 1024 * q + x, 1024 * q + 1024, 16), x == 0, x == 15)
+                mm(P(k, c, c + 64), R(w, 128 * x, 128 * x + 128), R("cand", 1024 * q + x, 1024 * q + 1024, 16), x == 0, x == 15)
 
     owners = [(rank + 1 + i) % N for i in range(N)]
 
-    def classify(k, c, n, cs, ck):
+    def classify(k, c, n, cs, k2, ck):
         act(R("ab", c, c + n), P(k, cs, cs + n), F.Abs, bias=R("nmid"))
-        ts(R("dead", c, c + n), R("ab", c, c + n), R("hlf"), float(DEAD), A.is_gt, A.mult)
-        tt(R("zt", c, c + n), R("dead", c, c + n), P(k, ck, ck + n), A.add)
-        ts(R("z2", c, c + n), R("zt", c, c + n), DEAD + 3, None, A.bitwise_and)
-        z = "z2"
-        if n > 64:
-            z = "zb"
-            cp(R("zb", c, c + n), R("z2", c, c + n))
+        act(R("dead", c, c + n), R("ab", c, c + n), F.Relu, scale=R("qd"), bias=R("nhl"))
+        tt(R("zt", c, c + n), R("dead", c, c + n), P(k2, ck, ck + n), A.add)
+        ts(R("z2", c, c + n), R("zt", c, c + n), 2 ** 31 - DEAD + 3, None, A.bitwise_and)
+        cp(R("zb", c, c + n), R("z2", c, c + n))
         for i, p in enumerate(owners):
-            ts(R("ind", 256 * i + c, 256 * i + c + n), R(z, c, c + n), float(p), None, A.is_equal)
+            ts(R("ind", 256 * i + c, 256 * i + c + n), R("zb", c, c + n), float(p), None, A.is_equal)
 
-    def build(t, wid, later):
+    def build(t, wid, later, last):
         for q in (0, 1, 2):
             gather_y(q, wid)
         act(R("xv"), X(R("bk", 0, wid), R("lx", 128, 192)), F.Copy)
@@ -335,12 +340,13 @@ def rank_program(g, core, T, topo):
         third(2, wid)
         sums(2)
         third(3, wid)
+        last()
         sums(3)
-        classify(0, 0, 192, 0, 192)
-        classify(1, 192, 64, 0, 64)
+        classify(0, 0, 128, 0, 0, 128)
+        classify(1, 128, 128, 0, 6, 128)
 
     def send(t, gap1, gap2, gap3):
-        win, arr, snd = "win%d" % t, "arr%d" % t, "snd%d" % t
+        win, wib, arr, snd = "win%d" % t, "wib%d" % t, "arr%d" % t, "snd%d" % t
         listify(P(4, 0, 64), "onx", "ind", 1024, True, True)
         gap1()
         cp(R("clb"), P(4, 0, 64))
@@ -351,29 +357,32 @@ def rank_program(g, core, T, topo):
         mm(P(5, 0, 64), R("blk"), R("csb"), False, False)
         mm(P(5, 0, 64), R("idn"), R("e0"), False, True)
         tt(R("iv"), P(5, 0, 64), R("cap"), A.is_ge)
-        ts(R("t2"), P(5, 0, 64), 383.0, None, A.min)
-        tt(R("t1"), R("iv"), R("trx"), A.mult)
-        tt(R("t3"), R("t1"), R("t2"), A.max)
+        ts(P(7, 128, 192), P(5, 0, 64), 191.0, None, A.min)
+        tt(R("t1"), R("iv"), P(7, 64, 128), A.mult)
+        tt(R("t3"), R("t1"), P(7, 128, 192), A.max)
         cp(R("off"), R("t3"))
         for h in range(2):
             mm(P(2 + h, 0, 512), R("tri"), R("ind", 512 * h, 512 * h + 512), True, True)
+        scatter(R(win), R("off", 0, 32), R("vd"))
+        act(X(R(wib), R("off", 32, 64)), R("vdb"), F.Silu)
         for i in range(4):
             act(R("pref", PAIR * i + 1, PAIR * i + 257), P(2 + i // 2, 256 * (i % 2), 256 * (i % 2) + 256), F.Copy)
-        scatter(R(win), R("off"), R("vd"))
-        ts(R("ns"), R(win, 0, 384), 0.0, None, A.is_equal)
-        scan(R("c1"), R("ns"), R(win, 0, 384), A.mult, A.add)
+        for i, w in enumerate((win, wib)):
+            ts(R("ns", 192 * i, 192 * i + 192), R(w, 0, 192), 0.0, None, A.is_equal)
+            scan(R("c1", 192 * i, 192 * i + 192), R("ns", 192 * i, 192 * i + 192), R(w, 0, 192), A.mult, A.add)
         mm(P(5, 64, 88), R("blk"), R("p272"), True, False)
         listify(P(5, 64, 88), "onx", "c1", 384, False, True)
         scan(R("cnt"), R("ns"), R("one"), A.mult, A.add)
         gap2()
-        ts(R("po"), P(5, 64, 88), 1.0 / 16, None, A.mult)
+        ts(R("po"), P(5, 64, 88), 1.0 / (16 * UNIT), None, A.mult)
         mm(P(6, 0, 24), R("blk"), R("mone"), True, False)
         listify(P(6, 0, 24), "onx", "c1", 384, False, False)
         tt(R("ll"), X(R("pref"), R("po")), R("cnt"), A.is_lt)
         gap3()
         listify(P(6, 0, 24), "lwx", "ll", 384, False, True)
-        ts(R("jl"), P(6, 0, 24), float(J), None, A.min)
-        cp(R(snd), X(R("cand"), R("jl", 0, 18)))
+        ts(R("jl"), P(6, 0, 24), 1.0 / UNIT, float(J), A.mult, A.min)
+        cp(R(snd, 0, 192), X(R("cand"), R("jl", 0, 12)))
+        act(R(snd, 192, 288), X(R("cand"), R("jl", 12, 18)), F.Copy)
         mine = plan(core, cores, topo)
         src = [R(snd, CAP * i, CAP * i + CAP) for i in range(N - 1)]
         prepare("g", [], [x for s in src for x in s[1]])
@@ -384,7 +393,7 @@ def rank_program(g, core, T, topo):
             tr.append(RemoteDMATransfer(dst_ids=[DstId(rid=rid, pnc=pid)], dma_engine_mask=sum(1 << e for e in mine[d]),
                                         remote_sem=T.sem["arrv%d" % t], src=src[i][0], dst=T[arr][:, CAP * rank:CAP * rank + CAP]))
         g.remote_dma_fused(tr, local_sem=T.sem["snt%d" % t])
-        cp(R(arr, CAP * rank, CAP * rank + CAP), X(R("cand"), R("jl", 18, 24)))
+        act(R(arr, CAP * rank, CAP * rank + CAP), X(R("cand"), R("jl", 18, 24)), F.Copy)
         total = sum(len(plan(c, cores, topo)[core]) for c in cores if c != core)
         order[0] += 1
         tok = {"n": order[0], "sem": "arrv%d" % t, "val": total, "q": "r", "snap": {}}
@@ -402,34 +411,35 @@ def rank_program(g, core, T, topo):
         cp(R("ki"), P(3, 0, 24))
         cp(R("r16"), R("r33"))
         ts(R("kb"), R("ki"), INV + 16383, None, A.bitwise_and)
-        ts(R("kb2"), R("kb"), 2, None, A.arith_shift_right)
         cp(R("kf"), R("kb"))
-        ts(R("bo"), R("kb2"), J, None, A.min)
-        cp(R("us"), X(R("tbl", 0, J + 16), R("bo")))
-        mm(P(0, 0, M), R("blk"), R("us"), True, False)
+        mm(P(0, 0, 16), R("blk"), R("z16"), True, True)
         for q in range(24):
             ts(R("eq", 400 * q, M * q + M), R("r16", 16 * q, M), R("kf", q, q + 1), None, A.is_equal)
+            if q == 0:
+                ts(R("kb2"), R("kb"), 2, None, A.arith_shift_right)
+            if q == 1:
+                ts(R("bo"), R("kb2"), J, None, A.min)
             if q < 23:
-                mm(P(0, 16 * q + 16, M), R("blk"), R("eq", 400 * q + 16, M * q + M), False, q == 22)
+                mm(P(0, 16 * q + 16, M), R("blk"), R("eq", 400 * q + 16, M * q + M), q == 0, q == 22)
         listify(P(1, 0, 24), "tx", "eq", 24 * M, True, False, 400)
-        cp(R("dm"), P(0, 0, M))
+        cp(R("us"), X(R("tbl", 0, J + 16), R("bo")))
+        tt(R("dm"), R("us"), P(0, 0, M), A.add)
         listify(P(1, 0, 24), "onx", "dm", M, False, True)
         ts(R("kp"), P(1, 0, 24), 0.0, None, A.is_equal)
-        ts(R("nk"), P(1, 0, 24), 0.0, None, A.is_gt)
         scan(R("ks"), R("one", 0, 24), R("kp"), A.mult, A.add)
-        tt(R("tn"), R("nk"), R("tk"), A.mult)
+        ts(R("nk"), P(1, 0, 24), 0.0, None, A.is_gt)
         if t == 0:
-            mm(P(7, 8, 9), R("blk"), R("ks", 23, 24), True, True)
+            mm(P(5, 100, 101), R("blk"), R("ks", 23, 24), True, True)
         mm(P(4, 64, 88), R("neg"), R("kp"), True, False)
         mm(P(4, 64, 88), R("blk"), R("ks"), False, True)
         if t == 0:
-            cp(R("n4"), P(7, 8, 9))
-            ts(R("wx"), R("n4"), R("nq", 0, 1), HALF, A.mult, A.add)
+            ts(R("wx"), P(5, 100, 101), R("nq", 0, 1), HALF, A.mult, A.add)
+            cp(R("n4"), P(5, 100, 101))
             ts(R("w0"), R("wx"), MAGIC, MAGIC, A.add, A.subtract)
+            ts(R("n4q"), R("n4"), 1.0 / 4096, None, A.mult)
             ts(R("scy1"), R("w0"), -8192.0, R("k1"), A.mult, A.subtract)
             ts(R("scx1"), R("w0"), 8192.0, R("k1"), A.mult, A.add)
-            ts(R("n4q"), R("n4"), 1.0 / 4096, None, A.mult)
-            ts(R("tq"), R("n4"), 1.0 / 4096, B / 4096.0, A.mult, A.add)
+        tt(R("tn"), R("nk"), R("tk"), A.mult)
         tt(R("om"), R("tn"), P(4, 64, 88), A.max)
         if base is None:
             cp(R("mo"), R("om"))
@@ -462,40 +472,41 @@ def rank_program(g, core, T, topo):
     sel(R("tri"), R("blk"), [[1, 128]], A.is_ge, 0, -1)
     sel(R("idn"), R("kib"), [[-1, 128]], A.is_equal, 0, 1)
     iota(R("cand", J, J + 16), [[0, 16]], -1)
-    iota(R("trx0"), [[16, 64]], 384)
+    iota(R("trx0"), [[0, 2], [16, 32]], 192)
     iota(R("rst"), [[0, 64]], 1)
-    iota(R("cap"), [[CAP, 4], [0, 16]], CAP)
-    iota(R("p6"), [[6, 4], [0, 16]], 0)
+    iota(R("cap"), [[0, 2], [CAP, 2], [0, 16]], CAP)
+    iota(R("p6"), [[0, 2], [6, 2], [0, 16]], 0)
     iota(R("rst", 0, 64, 16), [[0, 4]], 0)
-    iota(R("win0", 0, 384), [[0, 384]], 0)
-    iota(R("vd"), [[0, 4], [1, 256]], 1)
-    iota(R("win0", 0, 384, CAP), [[0, 4]], -1)
+    for w in ("win0", "wib0"):
+        iota(R(w, 0, 192), [[0, 192]], 0)
+    iota(R("vdb"), [[0, 2], [UNIT, 256]], UNIT)
+    iota(R("vd"), [[0, 2], [UNIT, 256]], UNIT)
+    for w in ("win0", "wib0"):
+        iota(R(w, 0, 192, CAP), [[0, 2]], -UNIT)
     iota(R("pref"), [[0, 4 * PAIR]], 0)
-    iota(R("p272"), [[PAIR, 4], [0, 6]], 0)
+    iota(R("p272"), [[UNIT * PAIR, 4], [0, 6]], 0)
     iota(R("one"), [[0, 384]], 1)
-    iota(R("mone"), [[0, 24]], -1)
+    iota(R("mone"), [[0, 24]], -UNIT)
     iota(R("tk0"), [[16, 24]], 2 * M)
     iota(R("tb0"), [[16, 24]], J + 16)
     sel(R("stri"), R("blk"), [[1, 128]], A.is_ge, -1, -1)
-    iota(R("tbl"), [[0, J + 16 + M]], 0)
+    iota(R("z16"), [[0, 16]], 0)
     iota(R("tx"), [[0, 2048]], 0)
-    iota(R("bk", B, B + 4 * M), [[0, 4 * M]], 0)
-    for h in ("hy1", "hx1"):
-        iota(R(h, 0, 1280, 5), [[0, 256]], -4096)
-    tt(R("mid"), R("sc", 4, 5), R("sc", 5, 6), A.add)
-    tt(R("hl0"), R("sc", 5, 6), R("sc", 4, 5), A.subtract)
-    ts(R("nmid"), R("mid"), -0.5, None, A.mult)
-    ts(R("hlf"), R("hl0"), 0.5, None, A.mult)
 
-    build(0, B, lambda: act(R("lwx"), R("onx"), F.Copy, scale=R("wl")))
+    def limits():
+        ts(R("nmid"), R("sc", 4, 5), R("sc", 5, 6), -0.5, A.add, A.mult)
+        ts(R("nhl"), R("sc", 5, 6), R("sc", 4, 5), -0.5 * DEAD, A.subtract, A.mult)
+        fill(R("qd"), float(DEAD))
+
+    build(0, B, lambda: act(R("lwx"), R("onx"), F.Silu, scale=R("wl")), limits)
 
     def gap0a():
-        ts(R("trx"), R("trx0"), R("rf"), None, A.add)
+        ts(P(7, 64, 128), R("trx0"), R("rf"), None, A.add)
         ts(R("tk"), R("tk0"), R("rf"), None, A.add)
         ts(R("kblk"), R("blk"), R("wk"), None, A.mult)
+        cp(R("lbf", 256, 512), R("lb", 256, 512))
 
     def gap0b():
-        cp(R("lbf", 256, 512), R("lb", 256, 512))
         fill(R("tbl", J, J + 16), 1)
         for k in range(4):
             affine(1, "y", k, 5)
@@ -503,41 +514,50 @@ def rank_program(g, core, T, topo):
     def gap0c():
         cp(R("laf", 256, 512), R("la", 256, 512))
         cp(R("lcf", 256, 512), R("lc", 256, 512))
-        for k in range(4):
-            affine(1, "x", k, 5)
 
     sent0, got0 = send(0, gap0a, gap0b, gap0c)
 
-    dma("y", "d_used", R("tbl", 0, J, rows=slice(0, 128, 16)), ext(T.used[:, :]))
+    for h in ("hy1", "hx1"):
+        iota(R(h, 0, 1280, 5), [[0, 256]], -4096)
+    iota(R("bk", B, B + 4 * M), [[0, 4 * M]], 0)
+    for k in range(4):
+        affine(1, "x", k, 5)
+    fill(R("q1"), 1.0 / 4096)
+    fill(R("b75"), B / 4096.0)
+    fill(R("bia"), BIAS)
+    fill(R("b4"), B + BIAS)
+    pairs(2, ((1, 3), (2, 2)))
+    ts(R("w", 2, 4), R("wq", 2, 4), MAGIC, MAGIC, A.add, A.subtract)
     spread("tx", "stri")
     for i in range(2):
-        iota(R("win1", 0, 384, CAP if i else 1), [[0, 4 if i else 384]], -i)
+        for w in ("win1", "wib1"):
+            iota(R(w, 0, 192, CAP if i else 1), [[0, 2 if i else 192]], -UNIT * i)
     ts(R("wb"), R("w", 2, 3), 2.0, R("w", 3, 4), A.mult, A.add)
     ts(R("by1", 1, 2), R("w", 3, 4), -8388608.0, -2048.0, A.mult, A.add)
     ts(R("by1", 2, 3), R("w", 3, 4), 8388608.0, -2048.0, A.mult, A.add)
     ts(R("k1"), R("wb"), 4096.0, None, A.mult)
     ts(R("by1", 0, 1), R("wb"), -8388608.0, -2048.0, A.mult, A.add)
     ts(R("by1", 3, 4), R("wb"), 8388608.0, -2048.0, A.mult, A.add)
-    ts(R("ur"), R("rf"), 0.0, None, A.is_equal)
     ts(R("bx1"), R("by1"), -1.0, None, A.mult)
 
     keep(0, None)
 
     for i in range(1, 5):
         hmask(1, "y", i, 5)
+    act(R("uy1", 0, 1280, 5), R("lbf", 256, 512), F.Identity, scale=R("n4q"), bias=R("b4"))
     act(R("ux1", 0, 1280, 5), R("laf", 256, 512), F.Identity, scale=R("n4q"), bias=R("b4"))
-    act(R("zf"), R("lcf", 256, 512), F.Identity, scale=R("tq"), bias=R("bia"))
     for i in range(1, 5):
         hmask(1, "x", i, 5)
+    act(R("tq"), R("n4"), F.Identity, scale=R("q1"), bias=R("b75"))
+    act(R("zf"), R("lcf", 256, 512), F.Identity, scale=R("tq"), bias=R("bia"))
     append(0)
-    ts(R("uy1", 0, 1280, 5), R("lb", 256, 512), R("n4q"), B + BIAS, A.mult, A.add)
     places(1, "y", 5)
     places(1, "x", 5)
     ts(R("lz"), R("zf"), MAGIC, MAGIC - MID, A.add, A.subtract)
-    build(1, B + M, lambda: None)
+    build(1, B + M, lambda: None, lambda: None)
 
     def gap1a():
-        ts(R("ud"), R("one"), R("ur"), None, A.mult)
+        cp(R("ud"), R("one"))
         ts(R("tb"), R("tb0"), R("rf"), None, A.add)
 
     def gap1b():
@@ -558,6 +578,6 @@ def rank_program(g, core, T, topo):
     g.wait_ge(T.sem.arrv0, got0)
     g.wait_ge(T.sem.arrv1, got1)
     for d in DMAS:
-        g.wait_ge(T.sem[d], 16)
+        g.wait_ge(T.sem[d], 256 if d == "d_used" else 16)
     for q in qsem:
         g.wait_ge(T.sem[qsem[q]], count[q])

from concourse.bass import DstId, RemoteDMATransfer
from concourse.mybir import AluOpType as A, ActivationFunctionType as F

F32, BF, I32, U16 = "float32", "bfloat16", "int32", "uint16"
B, J, CAP, N = 3072, 4096, 96, 4
M = N * CAP
MAGIC = 12582912.0
HALF = -2047.5 / 4096
MID = 1728
BIAS = HALF - MID
DEAD = 524288
PAIR = 272
INV = 1048576
UNIT = 32

SCRATCH = {}
ALIAS, COLS, SIZE = {}, {}, {F32: 0, BF: 0, I32: 0}
for _n, _c, _d in [
    ("nl", 8, I32), ("nf", 8, F32), ("sc", 8, F32), ("nq", 8, F32), ("cs4", 8, F32), ("ub", 8, F32), ("pr", 4, F32), ("wq", 4, F32), ("w", 4, F32),
    ("one8", 128, F32), ("b8a", 128, F32), ("b8", 128, F32), ("on4", 8, F32),
    ("pid", 1, I32), ("ri", 1, I32), ("rf", 1, F32), ("wk", 1, F32), ("wl0", 1, F32), ("wl", 1, F32),
    ("jc0", 256, F32), ("jc", 256, F32), ("trx0", 64, F32), ("tk0", 24, F32), ("tk", 24, F32), ("tb0", 24, F32), ("tb", 24, F32),
    ("ob", 128, BF), ("ba", 128, BF), ("blk", 128, BF), ("nb", 128, BF), ("nblk", 128, BF), ("tri", 128, BF), ("neg", 128, BF), ("stri", 128, BF),
    ("kib", 128, BF), ("idn", 128, BF), ("kblk", 128, BF), ("mob", 128, BF), ("idp", 128, BF), ("idm", 128, BF), ("z16", 16, BF),
    ("onx", 2048, BF), ("kwx", 2048, BF), ("lwx", 2048, BF), ("tx", 2048, BF),
    ("vd", 512, BF), ("vdb", 512, F32), ("rst", 64, BF), ("one", 384, BF), ("p6", 64, BF), ("cap", 64, F32), ("p272", 24, BF), ("mone", 24, BF), ("ud", 384, I32),
    ("nmid", 1, F32), ("nhl", 1, F32), ("qd", 1, F32), ("q1", 1, F32), ("b75", 1, F32), ("bia", 1, F32), ("b4", 1, F32),
    ("bx0", 4, F32), ("by0", 4, F32), ("bx1", 4, F32), ("by1", 4, F32), ("wb", 1, F32), ("k1", 1, F32),
    ("scx0", 1, F32), ("scy0", 1, F32), ("scx1", 1, F32), ("scy1", 1, F32),
    ("n4", 1, F32), ("n4q", 1, F32), ("tq", 1, F32), ("wx", 1, F32), ("w0", 1, F32),
    ("la", 512, I32), ("lb", 512, I32), ("lc", 512, I32), ("laf", 512, F32), ("lbf", 512, F32), ("lcf", 512, F32),
    ("ux0", 1024, F32), ("uy0", 1024, F32), ("ux1", 1280, F32), ("uy1", 1280, F32),
    ("hx0", 1024, BF), ("hy0", 1024, BF), ("hx1", 1280, BF), ("hy1", 1280, BF), ("sox", 1280, F32), ("soy", 1280, F32),
    ("zf", 256, F32), ("lx", 256, U16), ("ly", 256, U16), ("lz", 256, U16),
    ("bk", B + 4 * M, BF), ("yv", J, BF), ("xv", 1024, BF), ("fv", J, BF), ("cand", J + 16, BF),
    ("ab", 256, F32), ("dead", 256, F32), ("zt", 256, I32), ("z2", 256, I32), ("zb", 256, BF), ("ind", 1024, BF),
    ("clb", 64, BF), ("csb", 64, BF), ("e0", 64, BF), ("iv", 64, F32), ("t1", 64, F32), ("t3", 64, F32), ("off", 64, U16),
    ("win0", 704, BF), ("win1", 704, BF), ("wib0", 704, F32), ("wib1", 704, F32),
    ("ns", 384, BF), ("c1", 384, BF), ("cnt", 384, BF), ("po", 24, U16), ("pref", 4 * PAIR, BF),
    ("ll", 384, BF), ("jl", 24, U16), ("snd0", 288, BF), ("snd1", 288, BF), ("arr0", M, BF), ("arr1", M, BF),
    ("ki", 24, I32), ("kb", 24, I32), ("kf", 24, F32), ("kb2", 24, I32), ("bm", 24, F32), ("bo", 24, U16), ("r32", M, I32), ("r33", M, I32), ("r16", M, U16),
    ("tbl", J + 16 + M, I32), ("us", M, BF), ("eq", 24 * M, BF), ("dm", M, BF),
    ("nk", 24, BF), ("kp", 24, BF), ("ks", 24, BF), ("tn", 24, F32), ("om", 24, F32), ("mo", 24, U16), ("tn2", 24, F32), ("om2", 24, F32), ("mo2", 24, U16),
]:
    COLS[_n] = _c
    if _c <= 128 and _d != U16 and _n != "nl":
        ALIAS[_n] = ({F32: "pf", BF: "pb", I32: "pi"}[_d], SIZE[_d])
        SIZE[_d] += -(-_c // 8) * 8
    else:
        SCRATCH[_n] = ("sbuf", [128, _c], _d)
SCRATCH["pf"] = ("sbuf", [128, SIZE[F32]], F32)
SCRATCH["pb"] = ("sbuf", [128, SIZE[BF]], BF)
SCRATCH["pi"] = ("sbuf", [128, SIZE[I32]], I32)
for _n in range(8):
    SCRATCH["ps%d" % _n] = ("psum", [128, 512], F32)

DMAS = ["d_ncl", "d_lim", "d_la0", "d_lb0", "d_lc0", "d_la1", "d_lb1", "d_lc1", "d_bk", "d_used", "d_y"]
SEMAPHORES = ["cv", "cs", "ct", "cg", "arrv0", "arrv1", "snt0", "snt1"] + DMAS


def plan(src, cores, topo):
    own = topo.cores_of(src)
    far = [c for c in cores if c not in own]
    out = {}
    taken = []
    for i, d in enumerate(far):
        e = topo.engines(src, d)
        n = len(e) // len(far)
        out[d] = e[i * n:(i + 1) * n]
        taken += e
    for d in cores:
        if d in own and d != src:
            out[d] = [e for e in topo.engines(src, d) if e not in taken][:4]
    return out


def overlap(a, b):
    if a.start >= b.stop or b.start >= a.stop:
        return False
    if a.step == b.step and a.step > 1 and (a.start - b.start) % a.step:
        return False
    return True


def covers(a, b):
    return a.step == 1 and a.start <= b.start and b.stop <= a.stop


def rank_program(g, core, T, topo):
    rank = T.rank_of(core)
    if rank is None:
        return
    cores = list(T.cores)
    queues = {"v": g.vector, "s": g.scalar, "t": g.tensor, "g": g, "y": g.sync}
    qsem = {"v": "cv", "s": "cs", "t": "ct", "g": "cg"}
    count = {"v": 0, "s": 0, "t": 0, "g": 0}
    known = {q: {} for q in queues}
    wrote, read = {}, {}
    order = [0]

    def need(q, toks):
        for t in sorted(toks, key=lambda t: -t["n"]):
            if known[q].get(t["sem"], 0) < t["val"]:
                queues[q].wait_ge(T.sem[t["sem"]], t["val"])
                for k, v in t["snap"].items():
                    if known[q].get(k, 0) < v:
                        known[q][k] = v
                known[q][t["sem"]] = max(known[q].get(t["sem"], 0), t["val"])

    def prepare(q, outs, ins):
        toks = []
        for n, r in ins:
            for r2, t in wrote.get(n, []):
                if overlap(r, r2):
                    toks.append(t)
            if n.startswith("ps"):
                toks += [t for r2, t in wrote.get(n, []) + read.get(n, []) if t["q"] != q]
        for n, r in outs:
            ps = n.startswith("ps")
            for r2, t in wrote.get(n, []):
                if ps and t["q"] != q or (overlap(r, r2) and not (ps and q == "t")):
                    toks.append(t)
            for r2, t in read.get(n, []):
                if t["q"] != q and (ps or overlap(r, r2)):
                    toks.append(t)
        need(q, toks)

    def record(q, outs, ins, sem, val):
        order[0] += 1
        tok = {"n": order[0], "sem": sem, "val": val, "q": q, "snap": dict(known[q])}
        for n, r in outs:
            wrote[n] = [x for x in wrote.get(n, []) if not covers(r, x[0]) or n.startswith("ps")] + [(r, tok)]
            if not n.startswith("ps"):
                read[n] = [x for x in read.get(n, []) if not covers(r, x[0])]
        for n, r in ins:
            read[n] = [x for x in read.get(n, []) if not (x[1]["q"] == q and x[0] == r)] + [(r, tok)]
        for n, r in outs + ins:
            if n.startswith("ps"):
                for d in (wrote, read):
                    d[n] = list({(x[1]["q"], x[0].start, x[0].stop): x for x in d.get(n, [])}.values())

    def R(name, a=0, b=None, st=1, rows=None):
        b = COLS.get(name, 512) if b is None else b
        if name in ALIAS:
            name, o = ALIAS[name]
            a, b = a + o, b + o
        cols = slice(a, b) if st == 1 else slice(a, b, st)
        ap = T[name][:, cols] if rows is None else T[name][rows, cols]
        return (ap, [(name, range(a, b, st))])

    def X(w, o):
        return (w[0].indirect(o[0]), w[1] + o[1])

    def emit(q, outs, ins, f):
        prepare(q, outs, ins)
        inst = f(queues[q])
        count[q] += 1
        inst.then_inc(T.sem[qsem[q]], 1)
        record(q, outs, ins, qsem[q], count[q])

    def scal(x):
        return (x[0], x[1]) if isinstance(x, tuple) else (x, [])

    def ts(o, i, s1, s2, op0, op1=None):
        a, ra_ = scal(s1)
        b, rb_ = scal(s2)
        if op1 is None:
            emit("v", o[1], i[1] + ra_, lambda e: e.tensor_scalar(o[0], i[0], a, None, op0))
        else:
            emit("v", o[1], i[1] + ra_ + rb_, lambda e: e.tensor_scalar(o[0], i[0], a, b, op0, op1))

    def tt(o, a, b, op):
        emit("v", o[1], a[1] + b[1], lambda e: e.tensor_tensor(o[0], a[0], b[0], op))

    def cp(o, i):
        emit("v", o[1], i[1], lambda e: e.tensor_copy(o[0], i[0]))

    def scatter(w, o, i):
        emit("v", w[1], i[1] + o[1], lambda e: e.tensor_copy(w[0].indirect(o[0]), i[0]))

    def scan(o, a, b, op0, op1):
        emit("v", o[1], a[1] + b[1], lambda e: e.tensor_tensor_scan(o[0], a[0], b[0], 0.0, op0, op1))

    def fill(o, c):
        emit("v", o[1], [], lambda e: e.memset(o[0], c))

    def act(o, i, func, scale=None, bias=None):
        kw, more = {}, []
        for k, x in (("scale", scale), ("bias", bias)):
            if x is not None:
                kw[k] = x[0]
                more = more + x[1]
        emit("s", o[1], i[1] + more, lambda e: e.activation(o[0], i[0], func, **kw))

    def mm(o, l, r, start, stop):
        emit("t", o[1], l[1] + r[1], lambda e: e.matmul(o[0], l[0], r[0], start, stop))

    def iota(o, pattern, base, cm=0):
        emit("g", o[1], [], lambda e: e.iota(o[0], pattern, base, cm, allow_small_or_imprecise_dtypes=True))

    def sel(o, i, pattern, op, base, cm):
        emit("g", o[1], i[1], lambda e: e.affine_select(o[0], i[0], pattern, op, 0.0, base, cm))

    def dma(q, sem, o, i, total=16):
        if total == 16:
            prepare(q, o[1], i[1])
        queues[q].dma_start(o[0], i[0]).then_inc(T.sem[sem], 16)
        record(q, o[1], i[1], sem, total)

    def ext(ap):
        return (ap, [])

    def listify(o, wname, src, ncols, start, stop, st=16):
        for x in range(16):
            mm(o, R(wname, 128 * x, 128 * x + 128), R(src, x, ncols, st), start and x == 0, stop and x == 15)

    def P(k, a, b):
        return R("ps%d" % k, a, b)

    def spread(name, src, xs=range(16)):
        for x in xs:
            act(R(name, 129 * x, 128 * x + 128, 16), R(src, x, 128, 16), F.Copy)

    first8 = slice(0, 8)
    dma("y", "d_ncl", R("nl", 0, 4, rows=first8), ext(T.ncl[:, :]))
    dma("s", "d_lim", R("nl", 4, 6, rows=first8), ext(T.lim[:, :]))
    dma("y", "d_lb0", R("lb", 0, 256), ext(T.rb[:, 0:256]))
    dma("s", "d_la0", R("la", 0, 256), ext(T.ra[:, 0:256]))
    dma("y", "d_lc0", R("lc", 0, 256), ext(T.rc[:, 0:256]))
    dma("y", "d_bk", R("bk", 0, B), ext(T.bank[:, :]))
    dma("y", "d_lb1", R("lb", 256, 512), ext(T.rb[:, 256:512]))
    dma("y", "d_la1", R("la", 256, 512), ext(T.ra[:, 256:512]))
    dma("y", "d_lc1", R("lc", 256, 512), ext(T.rc[:, 256:512]))
    for r in range(16):
        dma("y", "d_used", R("tbl", 0, J, rows=slice(r, 128, 16)), ext(T.used[:, :]), 256)

    fill(R("ob"), 1.0)
    fill(R("one8"), 1.0)
    iota(R("pid"), [[0, 1]], 0, 1)
    ts(R("ri"), R("pid"), 15, None, A.bitwise_and)
    cp(R("rf"), R("ri"))
    fill(R("onx"), 0.0)
    ts(R("wk"), R("rf"), 14.0, 9.0, A.mult, A.add)
    ts(R("wl0"), R("rf"), 15.0, 8191.0 * UNIT, A.is_equal, A.mult)
    sel(R("ba"), R("ob"), [[-16, 8], [0, 16]], A.is_ge, 0, 1)
    sel(R("blk"), R("ba"), [[16, 8], [0, 16]], A.is_ge, 15, -1)
    sel(R("b8a", rows=first8), R("one8", rows=first8), [[1, 128]], A.is_ge, 0, -16)
    sel(R("b8", rows=first8), R("b8a", rows=first8), [[-1, 128]], A.is_ge, 15, 16)
    iota(R("jc0"), [[16, 256]], -2048)
    for h in ("hy0", "hx0"):
        iota(R(h, 0, 1024, 4), [[0, 256]], -4096)
    spread("onx", "blk", range(10))

    cp(R("nf", 0, 6, rows=first8), R("nl", 0, 6, rows=first8))
    mm(P(7, 0, 6), R("b8", rows=first8), R("nf", 0, 6, rows=first8), True, True)
    for x in range(10, 16):
        cp(R("onx", 129 * x, 128 * x + 128, 16), R("blk", x, 128, 16))
    act(R("kwx"), R("onx"), F.Copy, scale=R("wk"))
    cp(R("sc", 0, 6), P(7, 0, 6))

    def pairs(k, ab):
        for i, (a, b) in enumerate(ab):
            tt(R("pr", k + i, k + i + 1), R("sc", a, a + 1), R("sc", b, b + 1), A.mult)
        ts(R("wq", k, k + 2), R("pr", k, k + 2), 1.0 / 4096, HALF, A.mult, A.add)

    pairs(0, ((0, 3), (1, 2)))
    ts(R("jc"), R("jc0"), R("rf"), None, A.add)
    ts(R("w", 0, 2), R("wq", 0, 2), MAGIC, MAGIC, A.add, A.subtract)
    fill(R("by0", 1, 2), -2048.0)
    fill(R("on4"), 1.0)
    ts(R("by0", 0, 1), R("w", 1, 2), -16777216.0, -2048.0, A.mult, A.add)
    ts(R("by0", 2, 3), R("w", 1, 2), 16777216.0, -2048.0, A.mult, A.add)
    ts(R("scy0"), R("w", 0, 1), R("w", 1, 2), -8192.0, A.add, A.mult)
    ts(R("nq", 0, 4), R("sc", 0, 4), 1.0 / 4096, None, A.mult)
    scan(R("cs4", 0, 4), R("on4", 0, 4), R("sc", 0, 4), A.mult, A.add)
    fill(R("ub", 0, 1), BIAS)
    ts(R("scx0"), R("w", 0, 1), R("w", 1, 2), 8192.0, A.add, A.mult)
    ts(R("ub", 1, 4), R("cs4", 0, 3), BIAS, None, A.add)
    ts(R("wl"), R("wl0"), float(UNIT), None, A.add)
    ts(R("bx0", 0, 3), R("by0", 0, 3), -1.0, None, A.mult)

    def affine(t, who, k, s):
        i = s - 1 - k
        act(R("u%s%d" % (who, t), i, 256 * s, s), R("l%sf" % ("a" if who == "x" else "b"), 256 * t, 256 * t + 256), F.Identity,
            scale=R("nq", k, k + 1), bias=R("ub", k, k + 1))

    def hmask(t, who, i, s):
        k = s - 1 - i if who == "x" else i - 1
        act(R("h%s%d" % (who, t), i, 256 * s, s), R("jc"), F.Identity, scale=R("sc%s%d" % (who, t)), bias=R("b%s%d" % (who, t), k, k + 1))

    def places(t, who, s):
        o = "so" + who
        scan(R(o, 0, 256 * s), R("h%s%d" % (who, t)), R("u%s%d" % (who, t)), A.min, A.max)
        ts(R("l" + who), R(o, s - 1, 256 * s, s), MAGIC, MAGIC - MID, A.add, A.subtract)

    def gather_y(q, wid):
        act(R("yv", 1024 * q, 1024 * q + 1024), X(R("bk", 0, wid), R("ly", 64 * q, 64 * q + 64)), F.Copy)

    def first(q, wid):
        tt(R("fv", 1024 * q, 1024 * q + 1024), X(R("bk", 0, wid), R("lx", 64 * q, 64 * q + 64)), R("yv", 1024 * q, 1024 * q + 1024),
           (A.min, A.max, None, A.add)[q])

    def third(q, wid):
        tt(R("cand", 1024 * q, 1024 * q + 1024), X(R("bk", 0, wid), R("lz", 64 * q, 64 * q + 64)), R("fv", 1024 * q, 1024 * q + 1024), A.min)

    def sums(q):
        o = ((0, 64 * q), (0, 128 + 64 * q)) if q < 2 else ((1, 64 * q - 128), (6, 64 * q))
        for w, (k, c) in zip(("onx", "kwx"), o):
            for x in range(16):
                mm(P(k, c, c + 64), R(w, 128 * x, 128 * x + 128), R("cand", 1024 * q + x, 1024 * q + 1024, 16), x == 0, x == 15)

    owners = [(rank + 1 + i) % N for i in range(N)]

    def classify(k, c, n, cs, k2, ck):
        act(R("ab", c, c + n), P(k, cs, cs + n), F.Abs, bias=R("nmid"))
        act(R("dead", c, c + n), R("ab", c, c + n), F.Relu, scale=R("qd"), bias=R("nhl"))
        tt(R("zt", c, c + n), R("dead", c, c + n), P(k2, ck, ck + n), A.add)
        ts(R("z2", c, c + n), R("zt", c, c + n), 2 ** 31 - DEAD + 3, None, A.bitwise_and)
        cp(R("zb", c, c + n), R("z2", c, c + n))
        for i, p in enumerate(owners):
            ts(R("ind", 256 * i + c, 256 * i + c + n), R("zb", c, c + n), float(p), None, A.is_equal)

    def build(t, wid, later, last):
        for q in (0, 1, 2):
            gather_y(q, wid)
        act(R("xv"), X(R("bk", 0, wid), R("lx", 128, 192)), F.Copy)
        first(0, wid)
        gather_y(3, wid)
        third(0, wid)
        sums(0)
        for h in range(2):
            mm(P(2 + h, 0, 512), R("idp"), R("xv", 512 * h, 512 * h + 512), True, False)
            mm(P(2 + h, 0, 512), R("idm"), R("yv", 2048 + 512 * h, 2560 + 512 * h), False, True)
            act(R("fv", 2048 + 512 * h, 2560 + 512 * h), P(2 + h, 0, 512), F.Abs)
        later()
        first(1, wid)
        third(1, wid)
        sums(1)
        first(3, wid)
        third(2, wid)
        sums(2)
        third(3, wid)
        last()
        sums(3)
        classify(0, 0, 128, 0, 0, 128)
        classify(1, 128, 128, 0, 6, 128)

    def send(t, gap1, gap2, gap3):
        win, wib, arr, snd = "win%d" % t, "wib%d" % t, "arr%d" % t, "snd%d" % t
        listify(P(4, 0, 64), "onx", "ind", 1024, True, True)
        gap1()
        cp(R("clb"), P(4, 0, 64))
        scan(R("csb"), R("rst"), R("clb"), A.mult, A.add)
        ts(R("e0"), R("clb"), 0.0, None, A.is_equal)
        mm(P(5, 0, 64), R("blk"), R("p6"), True, False)
        mm(P(5, 0, 64), R("neg"), R("clb"), False, False)
        mm(P(5, 0, 64), R("blk"), R("csb"), False, False)
        mm(P(5, 0, 64), R("idn"), R("e0"), False, True)
        tt(R("iv"), P(5, 0, 64), R("cap"), A.is_ge)
        ts(P(7, 128, 192), P(5, 0, 64), 191.0, None, A.min)
        tt(R("t1"), R("iv"), P(7, 64, 128), A.mult)
        tt(R("t3"), R("t1"), P(7, 128, 192), A.max)
        cp(R("off"), R("t3"))
        for h in range(2):
            mm(P(2 + h, 0, 512), R("tri"), R("ind", 512 * h, 512 * h + 512), True, True)
        scatter(R(win), R("off", 0, 32), R("vd"))
        act(X(R(wib), R("off", 32, 64)), R("vdb"), F.Silu)
        for i in range(4):
            act(R("pref", PAIR * i + 1, PAIR * i + 257), P(2 + i // 2, 256 * (i % 2), 256 * (i % 2) + 256), F.Copy)
        for i, w in enumerate((win, wib)):
            ts(R("ns", 192 * i, 192 * i + 192), R(w, 0, 192), 0.0, None, A.is_equal)
            scan(R("c1", 192 * i, 192 * i + 192), R("ns", 192 * i, 192 * i + 192), R(w, 0, 192), A.mult, A.add)
        mm(P(5, 64, 88), R("blk"), R("p272"), True, False)
        listify(P(5, 64, 88), "onx", "c1", 384, False, True)
        scan(R("cnt"), R("ns"), R("one"), A.mult, A.add)
        gap2()
        ts(R("po"), P(5, 64, 88), 1.0 / (16 * UNIT), None, A.mult)
        mm(P(6, 0, 24), R("blk"), R("mone"), True, False)
        listify(P(6, 0, 24), "onx", "c1", 384, False, False)
        tt(R("ll"), X(R("pref"), R("po")), R("cnt"), A.is_lt)
        gap3()
        listify(P(6, 0, 24), "lwx", "ll", 384, False, True)
        ts(R("jl"), P(6, 0, 24), 1.0 / UNIT, float(J), A.mult, A.min)
        cp(R(snd, 0, 192), X(R("cand"), R("jl", 0, 12)))
        act(R(snd, 192, 288), X(R("cand"), R("jl", 12, 18)), F.Copy)
        mine = plan(core, cores, topo)
        src = [R(snd, CAP * i, CAP * i + CAP) for i in range(N - 1)]
        prepare("g", [], [x for s in src for x in s[1]])
        tr = []
        for i in range(N - 1):
            d = cores[owners[i]]
            rid, pid = topo.addr(d, core)
            tr.append(RemoteDMATransfer(dst_ids=[DstId(rid=rid, pnc=pid)], dma_engine_mask=sum(1 << e for e in mine[d]),
                                        remote_sem=T.sem["arrv%d" % t], src=src[i][0], dst=T[arr][:, CAP * rank:CAP * rank + CAP]))
        g.remote_dma_fused(tr, local_sem=T.sem["snt%d" % t])
        act(R(arr, CAP * rank, CAP * rank + CAP), X(R("cand"), R("jl", 18, 24)), F.Copy)
        total = sum(len(plan(c, cores, topo)[core]) for c in cores if c != core)
        order[0] += 1
        tok = {"n": order[0], "sem": "arrv%d" % t, "val": total, "q": "r", "snap": {}}
        for q in range(N):
            if q != rank:
                wrote.setdefault(arr, []).append((range(CAP * q, CAP * q + CAP), tok))
        return sum(len(e) for e in mine.values()), total

    def keep(t, base):
        arr = "arr%d" % t
        mm(P(2, 0, M), R("kblk"), R(arr), True, True)
        listify(P(3, 0, 24), "kwx", arr, M, True, True)
        cp(R("r32"), P(2, 0, M))
        ts(R("r33"), R("r32"), INV + 16383, None, A.bitwise_and)
        cp(R("ki"), P(3, 0, 24))
        cp(R("r16"), R("r33"))
        ts(R("kb"), R("ki"), INV + 16383, None, A.bitwise_and)
        cp(R("kf"), R("kb"))
        mm(P(0, 0, 16), R("blk"), R("z16"), True, True)
        for q in range(24):
            ts(R("eq", 400 * q, M * q + M), R("r16", 16 * q, M), R("kf", q, q + 1), None, A.is_equal)
            if q == 0:
                ts(R("kb2"), R("kb"), 2, None, A.arith_shift_right)
            if q == 1:
                ts(R("bo"), R("kb2"), J, None, A.min)
            if q < 23:
                mm(P(0, 16 * q + 16, M), R("blk"), R("eq", 400 * q + 16, M * q + M), q == 0, q == 22)
        listify(P(1, 0, 24), "tx", "eq", 24 * M, True, False, 400)
        cp(R("us"), X(R("tbl", 0, J + 16), R("bo")))
        tt(R("dm"), R("us"), P(0, 0, M), A.add)
        listify(P(1, 0, 24), "onx", "dm", M, False, True)
        ts(R("kp"), P(1, 0, 24), 0.0, None, A.is_equal)
        scan(R("ks"), R("one", 0, 24), R("kp"), A.mult, A.add)
        ts(R("nk"), P(1, 0, 24), 0.0, None, A.is_gt)
        if t == 0:
            mm(P(5, 100, 101), R("blk"), R("ks", 23, 24), True, True)
        mm(P(4, 64, 88), R("neg"), R("kp"), True, False)
        mm(P(4, 64, 88), R("blk"), R("ks"), False, True)
        if t == 0:
            ts(R("wx"), P(5, 100, 101), R("nq", 0, 1), HALF, A.mult, A.add)
            cp(R("n4"), P(5, 100, 101))
            ts(R("w0"), R("wx"), MAGIC, MAGIC, A.add, A.subtract)
            ts(R("n4q"), R("n4"), 1.0 / 4096, None, A.mult)
            ts(R("scy1"), R("w0"), -8192.0, R("k1"), A.mult, A.subtract)
            ts(R("scx1"), R("w0"), 8192.0, R("k1"), A.mult, A.add)
        tt(R("tn"), R("nk"), R("tk"), A.mult)
        tt(R("om"), R("tn"), P(4, 64, 88), A.max)
        if base is None:
            cp(R("mo"), R("om"))
        else:
            ts(R("mo"), R("om"), base, None, A.add)

    def append(t):
        scatter(R("bk", B, B + 4 * M), R("mo"), R("arr%d" % t))

    for i in range(1, 4):
        hmask(0, "y", i, 4)
    for i in range(1, 4):
        hmask(0, "x", i, 4)
    cp(R("laf", 0, 256), R("la", 0, 256))
    for k in range(4):
        affine(0, "x", k, 4)
    for k in range(4):
        ts(R("uy0", 3 - k, 1024, 4), R("lb", 0, 256), R("nq", k, k + 1), R("ub", k, k + 1), A.mult, A.add)
    places(0, "y", 4)
    places(0, "x", 4)
    ts(R("zf"), R("lc", 0, 256), B / 4096.0, BIAS, A.mult, A.add)
    ts(R("lz"), R("zf"), MAGIC, MAGIC - MID, A.add, A.subtract)
    iota(R("mob"), [[0, 128]], -1)
    iota(R("kib"), [[0, 128]], 1024)
    sel(R("idp"), R("ob"), [[-1, 128]], A.is_equal, 0, 1)
    sel(R("idm"), R("mob"), [[-1, 128]], A.is_equal, 0, 1)
    sel(R("nb"), R("mob"), [[-16, 8], [0, 16]], A.is_ge, 0, 1)
    sel(R("nblk"), R("nb"), [[16, 8], [0, 16]], A.is_ge, 15, -1)
    sel(R("neg"), R("nblk"), [[-1, 128]], A.is_ge, 0, 1)
    sel(R("tri"), R("blk"), [[1, 128]], A.is_ge, 0, -1)
    sel(R("idn"), R("kib"), [[-1, 128]], A.is_equal, 0, 1)
    iota(R("cand", J, J + 16), [[0, 16]], -1)
    iota(R("trx0"), [[0, 2], [16, 32]], 192)
    iota(R("rst"), [[0, 64]], 1)
    iota(R("cap"), [[0, 2], [CAP, 2], [0, 16]], CAP)
    iota(R("p6"), [[0, 2], [6, 2], [0, 16]], 0)
    iota(R("rst", 0, 64, 16), [[0, 4]], 0)
    for w in ("win0", "wib0"):
        iota(R(w, 0, 192), [[0, 192]], 0)
    iota(R("vdb"), [[0, 2], [UNIT, 256]], UNIT)
    iota(R("vd"), [[0, 2], [UNIT, 256]], UNIT)
    for w in ("win0", "wib0"):
        iota(R(w, 0, 192, CAP), [[0, 2]], -UNIT)
    iota(R("pref"), [[0, 4 * PAIR]], 0)
    iota(R("p272"), [[UNIT * PAIR, 4], [0, 6]], 0)
    iota(R("one"), [[0, 384]], 1)
    iota(R("mone"), [[0, 24]], -UNIT)
    iota(R("tk0"), [[16, 24]], 2 * M)
    iota(R("tb0"), [[16, 24]], J + 16)
    sel(R("stri"), R("blk"), [[1, 128]], A.is_ge, -1, -1)
    iota(R("z16"), [[0, 16]], 0)
    iota(R("tx"), [[0, 2048]], 0)

    def limits():
        ts(R("nmid"), R("sc", 4, 5), R("sc", 5, 6), -0.5, A.add, A.mult)
        ts(R("nhl"), R("sc", 5, 6), R("sc", 4, 5), -0.5 * DEAD, A.subtract, A.mult)
        fill(R("qd"), float(DEAD))

    build(0, B, lambda: act(R("lwx"), R("onx"), F.Silu, scale=R("wl")), limits)

    def gap0a():
        ts(P(7, 64, 128), R("trx0"), R("rf"), None, A.add)
        ts(R("tk"), R("tk0"), R("rf"), None, A.add)
        ts(R("kblk"), R("blk"), R("wk"), None, A.mult)
        cp(R("lbf", 256, 512), R("lb", 256, 512))

    def gap0b():
        fill(R("tbl", J, J + 16), 1)
        for k in range(4):
            affine(1, "y", k, 5)

    def gap0c():
        cp(R("laf", 256, 512), R("la", 256, 512))
        cp(R("lcf", 256, 512), R("lc", 256, 512))

    sent0, got0 = send(0, gap0a, gap0b, gap0c)

    for h in ("hy1", "hx1"):
        iota(R(h, 0, 1280, 5), [[0, 256]], -4096)
    iota(R("bk", B, B + 4 * M), [[0, 4 * M]], 0)
    for k in range(4):
        affine(1, "x", k, 5)
    fill(R("q1"), 1.0 / 4096)
    fill(R("b75"), B / 4096.0)
    fill(R("bia"), BIAS)
    fill(R("b4"), B + BIAS)
    pairs(2, ((1, 3), (2, 2)))
    ts(R("w", 2, 4), R("wq", 2, 4), MAGIC, MAGIC, A.add, A.subtract)
    spread("tx", "stri")
    for i in range(2):
        for w in ("win1", "wib1"):
            iota(R(w, 0, 192, CAP if i else 1), [[0, 2 if i else 192]], -UNIT * i)
    ts(R("wb"), R("w", 2, 3), 2.0, R("w", 3, 4), A.mult, A.add)
    ts(R("by1", 1, 2), R("w", 3, 4), -8388608.0, -2048.0, A.mult, A.add)
    ts(R("by1", 2, 3), R("w", 3, 4), 8388608.0, -2048.0, A.mult, A.add)
    ts(R("k1"), R("wb"), 4096.0, None, A.mult)
    ts(R("by1", 0, 1), R("wb"), -8388608.0, -2048.0, A.mult, A.add)
    ts(R("by1", 3, 4), R("wb"), 8388608.0, -2048.0, A.mult, A.add)
    ts(R("bx1"), R("by1"), -1.0, None, A.mult)

    keep(0, None)

    for i in range(1, 5):
        hmask(1, "y", i, 5)
    act(R("uy1", 0, 1280, 5), R("lbf", 256, 512), F.Identity, scale=R("n4q"), bias=R("b4"))
    act(R("ux1", 0, 1280, 5), R("laf", 256, 512), F.Identity, scale=R("n4q"), bias=R("b4"))
    for i in range(1, 5):
        hmask(1, "x", i, 5)
    act(R("tq"), R("n4"), F.Identity, scale=R("q1"), bias=R("b75"))
    act(R("zf"), R("lcf", 256, 512), F.Identity, scale=R("tq"), bias=R("bia"))
    append(0)
    places(1, "y", 5)
    places(1, "x", 5)
    ts(R("lz"), R("zf"), MAGIC, MAGIC - MID, A.add, A.subtract)
    build(1, B + M, lambda: None, lambda: None)

    def gap1a():
        cp(R("ud"), R("one"))
        ts(R("tb"), R("tb0"), R("rf"), None, A.add)

    def gap1b():
        ts(R("bm"), R("kb2"), float(J), None, A.min)
        tt(R("tn2"), R("nk"), R("tb"), A.mult)
        tt(R("om2"), R("tn2"), R("bm"), A.max)
        cp(R("mo2"), R("om2"))

    sent1, got1 = send(1, gap1a, gap1b, lambda: None)
    scatter(R("tbl"), R("mo2"), R("ud"))

    keep(1, R("n4"))
    append(1)
    dma("y", "d_y", ext(T.y[:, :]), R("bk", B, B + 2 * M))

    g.wait_ge(T.sem.snt0, sent0)
    g.wait_ge(T.sem.snt1, sent1)
    g.wait_ge(T.sem.arrv0, got0)
    g.wait_ge(T.sem.arrv1, got1)
    for d in DMAS:
        g.wait_ge(T.sem[d], 256 if d == "d_used" else 16)
    for q in qsem:
        g.wait_ge(T.sem[qsem[q]], count[q])
